import numpy as np
import ml_dtypes


def mxq(x, axis, fmt="e4m3"):
    dtype, down = {"e4m3": (ml_dtypes.float8_e4m3fn, 7), "e5m2": (ml_dtypes.float8_e5m2, 14)}[fmt]
    v = np.moveaxis(np.asarray(x, np.float32).astype(ml_dtypes.bfloat16).astype(np.float64), axis, -1)
    blocks = v.reshape(v.shape[:-1] + (-1, 32))
    amax = np.abs(blocks).max(-1, keepdims=True)
    byte = np.maximum(np.where(amax > 0, np.frexp(amax)[1] - 1 + 127, 0) - down, 1)
    scale = np.exp2(byte - 127.0)
    codes = (blocks / scale).astype(np.float32).astype(dtype).astype(np.float64)
    return np.moveaxis((codes * scale).reshape(v.shape), -1, axis)


WIDE = False


def mx_kscale(k):
    if not WIDE:
        return np.ones(k)
    levels = np.array([24, -24, 12, -12, 0])
    if k % 512:
        return np.exp2(np.random.permutation(np.resize(levels, k // 32))).repeat(32)
    a = np.empty((k // 512, 16))
    for p in range(k // 512):
        a[p, :8] = np.random.permutation(np.resize(levels, 8))
        for g in range(8):
            far = levels[np.abs(levels - a[p, g]) >= 10]
            a[p, g + 8] = far[np.random.randint(len(far))]
    return np.exp2(a.ravel()).repeat(32)


def f64(x):
    return np.asarray(x).astype(np.float64)


def striped(idx):
    return np.tile(idx.reshape(-1, 16).T, (8, 1)).astype(np.uint16)


def unstriped(offs):
    return offs[:16].T.reshape(-1).astype(np.int64)


E2M1 = np.array([0.0, 0.5, 1.0, 1.5, 2.0, 3.0, 4.0, 6.0, -0.0, -0.5, -1.0, -1.5, -2.0, -3.0, -4.0, -6.0])


def pack_weight(w, fmt):
    k, n = w.shape
    w = f64(np.asarray(w, np.float32).astype(ml_dtypes.bfloat16)).reshape(k // 32, 32, n)
    amax = np.abs(w).max(1)
    if fmt == "e4m3":
        byte = np.frexp(amax)[1] - 1 + 127 - 7
    else:
        mant, ex = np.frexp(amax / 6.0)
        byte = np.where(mant > 0.5, ex, ex - 1) + 127
    byte = np.clip(np.where(amax > 0, byte, 1), 1, 254)
    scaled = (w * np.exp2(127.0 - byte)[:, None, :]).reshape(k, n).astype(np.float32)
    by_word = np.ascontiguousarray(scaled.reshape(k // 512, 128, 4, n).transpose(0, 1, 3, 2))
    if fmt == "e4m3":
        words = by_word.astype(ml_dtypes.float8_e4m3fn).view(np.uint8)
    else:
        c = by_word.astype(ml_dtypes.float4_e2m1fn).view(np.uint8) & 0xF
        words = (c[..., 0::2] | (c[..., 1::2] << 4)).reshape(k // 512, 128, 2 * n)
    return np.ascontiguousarray(words), np.ascontiguousarray(byte.astype(np.uint8).reshape(k // 512, 16, n))


def unpack_weight(words, scales, fmt):
    g, _, n = scales.shape
    words = np.ascontiguousarray(words).reshape(g, 128, n, -1)
    if fmt == "e4m3":
        vals = words.view(ml_dtypes.float8_e4m3fn).astype(np.float64)
    else:
        nib = np.empty((g, 128, n, 4), np.uint8)
        nib[..., 0::2] = words & 0xF
        nib[..., 1::2] = words >> 4
        vals = E2M1[nib]
    vals = vals * np.repeat(np.exp2(scales.astype(np.float64) - 127.0), 8, axis=1)[..., None]
    return vals.transpose(0, 1, 3, 2).reshape(g * 512, n)


K, R, N, T, J = 1536, 1024, 1024, 2048, 1024


def setup_inputs():
    n = np.random.standard_normal
    s = mx_kscale(K)[:, None]
    u = mx_kscale(R)[:, None]
    p_tab = pack_weight(n((K, T)) * s, "e4m3")
    p_wb = pack_weight(0.7 * n((K, N)) / np.sqrt(K) / s, "e4m3")
    p_dn = pack_weight(n((K, R)) / np.sqrt(K) / s * u.T, "e2m1")
    return {
        "tab_words": p_tab[0],
        "tab_scales": p_tab[1],
        "wb_words": p_wb[0],
        "wb_scales": p_wb[1],
        "dn_words": p_dn[0],
        "dn_scales": p_dn[1],
        "upw": (2.0 * n((R, N)) / np.sqrt(R) / u).astype(np.float32),
        "x0T": (n((N, T))).astype(np.float32),
        "b": (0.3 * n(N)).astype(np.float32),
        "offs": striped(np.random.permutation(T)[:J]),
    }


def reference(tab_words, tab_scales, wb_words, wb_scales, dn_words, dn_scales, upw, x0T, b, offs):
    idx = unstriped(offs)
    tab_ = unpack_weight(tab_words, tab_scales, "e4m3")[:, idx]
    wb_ = unpack_weight(wb_words, wb_scales, "e4m3")
    dn_ = unpack_weight(dn_words, dn_scales, "e2m1")
    hs = dn_.T @ tab_
    h = np.maximum(hs, 0.0)
    h_ = mxq(h, 0, "e4m3")
    upw_ = mxq(f64(upw), 0, "e4m3")
    y = wb_.T @ tab_ + upw_.T @ h_
    return f64(x0T)[:, idx] * (y + f64(b)[:, None]) + f64(x0T)[:, idx]

@@ -1,0 +1,252 @@
+from contextlib import ExitStack
+
+import concourse.mybir as mybir
+from concourse.masks import make_identity
+
+K, R, N, T, J = 1536, 1024, 1024, 2048, 1024
+FLOPS = 2 * J * (K * R + K * N + R * N)
+
+F32 = mybir.dt.float32
+BF16 = mybir.dt.bfloat16
+I32 = mybir.dt.int32
+U32 = mybir.dt.uint32
+U16 = mybir.dt.uint16
+U8 = mybir.dt.uint8
+FP8X4 = mybir.dt.float8_e4m3fn_x4
+FP4X4 = mybir.dt.float4_e2m1fn_x4
+ACT = mybir.ActivationFunctionType
+MULT = mybir.AluOpType.mult
+
+P = 128
+KP = K // 512
+RP = R // 512
+NT = N // P
+HALF = 512
+QUART = 256
+
+
+def tile_list_xcross_relu_kernel(
+    tc, tab_words, tab_scales, wb_words, wb_scales, dn_words, dn_scales, upw, x0T, b, offs, out
+):
+    nc = tc.nc
+    with ExitStack() as ctx:
+        keep = ctx.enter_context(tc.tile_pool(name="keep", bufs=1))
+        wide = ctx.enter_context(tc.tile_pool(name="wide", bufs=8))
+        ring = ctx.enter_context(tc.tile_pool(name="ring", bufs=3))
+        psum = ctx.enter_context(tc.psum_pool(name="psum", bufs=4))
+
+        def held(shape, dtype, name):
+            return keep.tile(shape, dtype, name=name, align_bytes=64)
+
+        def bank(side):
+            return psum.tile([P, HALF], F32, name="bank%d" % side)
+
+        offsets = keep.tile([P, J // 16], U16, name="offsets")
+        tab_plane = held([P, KP, T // 4], I32, "tab_plane")
+        dn_plane_raw = held([P, KP, R // 4], I32, "dn_plane_raw")
+        wb_plane = held([P, N // 4], I32, "wb_plane")
+        b_rows = held([P, P], F32, "b_rows")
+        ident = held([P, P], F32, "ident")
+
+        dn_raw01 = held([P, KP - 1, R // 2], I32, "dn_raw01")
+        dn_raw2 = held([P, R // 2], I32, "shared")
+        dn_raw = [dn_raw01[:, 0, :], dn_raw01[:, 1, :], dn_raw2[:]]
+        tab_win = [wide.tile([P, T], I32, name="window", align_bytes=64) for a in range(KP)]
+
+        def load_table(a):
+            nc.sync.dma_start(tab_win[a][:], tab_words[a].rearrange("p t i -> p (t i)").bitcast(I32))
+
+        def load_wb_plane(q):
+            nc.sync.dma_start(
+                wb_plane[32 * q : 32 * q + 4 * KP, :], wb_scales[:, 4 * q : 4 * q + 4, :].bitcast(I32)
+            )
+
+        tab_flat = tab_plane[:].rearrange("p a w -> p (a w)")
+        nc.gpsimd.memset(wb_plane[:], 0)
+        nc.vector.memset(tab_flat[:, 0:768], 0)
+        nc.gpsimd.memset(tab_flat[:, 768:1536], 0)
+        nc.vector.memset(dn_plane_raw[:], 0)
+        make_identity(nc, ident[:])
+        nc.sync.dma_start(offsets[:], offs)
+        nc.sync.dma_start(dn_raw01[:], dn_words[0:2].rearrange("a p w -> p a w").bitcast(I32))
+        nc.sync.dma_start(b_rows[:], b.rearrange("(c p) -> c p", p=P).unsqueeze(0).broadcast_to([P // NT, NT, P]))
+        load_wb_plane(0)
+        for q in range(4):
+            nc.sync.dma_start(
+                tab_plane[32 * q : 32 * q + 4],
+                tab_scales[:, 4 * q : 4 * q + 4, :].rearrange("a r t -> r a t").bitcast(I32),
+            )
+        load_table(0)
+        for q in range(4):
+            nc.sync.dma_start(
+                dn_plane_raw[32 * q : 32 * q + 4],
+                dn_scales[:, 4 * q : 4 * q + 4, :].rearrange("a r n -> r a n").bitcast(I32),
+            )
+        for a in range(1, KP):
+            load_table(a)
+        nc.sync.dma_start(dn_raw2[:], dn_words[2].bitcast(I32))
+        for q in range(1, 4):
+            load_wb_plane(q)
+        wb = held([P, KP, N], I32, "wb")
+        for a in range(KP):
+            nc.sync.dma_start(wb[:, a, :], wb_words[a].rearrange("p n i -> p (n i)").bitcast(I32))
+        up_raw = held([P, RP, 4, N], F32, "up_raw")
+        up_rows = upw.rearrange("(g q t i) n -> g t q i n", g=RP, q=16, t=4, i=8)
+        for g in range(RP):
+            for t in range(4):
+                nc.sync.dma_start(up_raw[:, g, t, :], up_rows[g, t])
+        x0 = []
+        for c in range(NT):
+            win = wide.tile([P, T], F32, name="window", align_bytes=64)
+            nc.sync.dma_start(win[:], x0T[c * P : (c + 1) * P, :])
+            x0.append(win)
+
+        b_t = bank(0)
+        nc.tensor.transpose(b_t[:, 0:P], b_rows[:], ident[:])
+        bias1 = held([P, NT], F32, "bias1")
+        nc.scalar.activation(bias1[:], b_t[:, 0:NT], ACT.Identity, bias=1.0)
+
+        dn = held([P, KP, RP, 4, 64], I32, "dn")
+        dn_plane = held([P, KP, RP, 4, 32], I32, "dn_plane")
+        v_half = []
+
+        def new_half(name):
+            v_half.append(held([P, KP * (HALF + HALF // 4)], U32, name))
+
+        def v_words(a, j0, width):
+            at = a * HALF + j0 % HALF
+            return v_half[j0 // HALF][:, at : at + width]
+
+        def v_plane(a, j0, width):
+            at = a * HALF + j0 % HALF
+            return v_half[j0 // HALF][:, KP * HALF :].bitcast(U8)[:, at : at + width]
+
+        def permute_dn(a):
+            for g in range(RP):
+                nc.vector.tensor_copy(
+                    dn[:, a, g].rearrange("p t (q w) -> p t q w", w=4),
+                    dn_raw[a][:, 256 * g : 256 * (g + 1)].rearrange("p (q t w) -> p t q w", t=4, w=4),
+                )
+                nc.vector.tensor_copy(
+                    dn_plane[:, a, g].rearrange("p t (q w) -> p t q w", w=2),
+                    dn_plane_raw[:, a, 128 * g : 128 * (g + 1)].rearrange("p (q t w) -> p t q w", t=4, w=2),
+                )
+
+        def listed(window, j0, width):
+            return window.indirect(offsets[:, j0 // 16 : (j0 + width) // 16])
+
+        def gather(a, j0, width):
+            nc.vector.tensor_copy(v_plane(a, j0, width), listed(tab_plane[:, a, :].bitcast(U8), j0, width))
+            nc.vector.tensor_copy(v_words(a, j0, width), listed(tab_win[a][:].bitcast(U32), j0, width))
+
+        def dn_pass(acc, a, g, t, j0, width):
+            nc.tensor.matmul_mx(
+                acc,
+                lhsT=dn[:, a, g, t, :].bitcast(FP4X4),
+                lhsT_scale=dn_plane[:, a, g, t, :].bitcast(U8),
+                rhs=v_words(a, j0, width).bitcast(FP8X4),
+                rhs_scale=v_plane(a, j0, width),
+                start=(a == 0),
+                stop=(a == KP - 1),
+            )
+
+        h_words = held([P, RP, J], U32, "h_words")
+        h_plane = held([P, RP, J], U8, "h_plane")
+
+        def quantise(words, plane, grouped):
+            nc.vector.quantize_mx(out=words.bitcast(FP8X4), scales=plane, in_=grouped.rearrange("p c t -> p (c t)"))
+
+        first = [[bank(g) for t in range(4)] for g in range(RP)]
+        new_half("v_first")
+        for a in range(KP):
+            permute_dn(a)
+            gather(a, 0, HALF)
+            for g in range(RP):
+                for t in range(4):
+                    dn_pass(first[g][t][:], a, g, t, 0, HALF)
+        h_flat = [held([P, 4, HALF], BF16, "h_flat%d" % g) for g in range(RP)]
+        for g in range(RP):
+            for t in range(4):
+                nc.scalar.activation(h_flat[g][:, t, :], first[g][t][:], ACT.Relu)
+
+        late = []
+        new_half("shared")
+        for j0 in range(HALF, J, QUART):
+            for a in range(KP):
+                gather(a, j0, QUART)
+            for g in range(RP):
+                grouped = ring.tile([P, QUART, 4], BF16, name="h_late", bufs=4, align_bytes=64)
+                for s in range(0, QUART, P):
+                    acc = bank(0)
+                    for t in range(4):
+                        for a in range(KP):
+                            dn_pass(acc[:, t * P : (t + 1) * P], a, g, t, j0 + s, P)
+                    nc.scalar.activation(
+                        grouped[:, s : s + P, :], acc[:].rearrange("p (t j) -> p j t", t=4), ACT.Relu
+                    )
+                late.append((g, j0, grouped))
+
+        early = []
+        for g in range(RP):
+            grouped = ring.tile([P, HALF, 4], BF16, name="h_early", bufs=2, align_bytes=64)
+            nc.vector.tensor_copy(
+                grouped[:].rearrange("p (c i) t -> p c t i", i=4),
+                h_flat[g][:].rearrange("p t (c i) -> p c t i", i=4),
+            )
+            early.append(grouped)
+        for g in range(RP):
+            quantise(h_words[:, g, 0:HALF], h_plane[:, g, 0:HALF], early[g][:])
+        for g, j0, grouped in late:
+            quantise(h_words[:, g, j0 : j0 + QUART], h_plane[:, g, j0 : j0 + QUART], grouped[:])
+
+        up_words = held([P, NT, RP, P], U32, "up_words")
+        up_plane = held([P, NT, RP, P], U8, "up_plane")
+
+        def quantise_up(c):
+            grouped = ring.tile([P, RP * P, 4], BF16, name="up_grouped", align_bytes=64)
+            for g in range(RP):
+                nc.scalar.copy(
+                    grouped[:, g * P : (g + 1) * P, :].rearrange("p (c i) t -> p c t i", i=4),
+                    up_raw[:, g, :, c * P : (c + 1) * P].rearrange("p t (c i) -> p c t i", i=4),
+                )
+            quantise(
+                up_words[:, c].rearrange("p g m -> p (g m)"), up_plane[:, c].rearrange("p g m -> p (g m)"), grouped[:]
+            )
+
+        wb_bytes = wb_plane[:].bitcast(U8)
+        quantise_up(0)
+        for c in range(NT):
+            cols = slice(c * P, (c + 1) * P)
+            if c + 1 < NT:
+                quantise_up(c + 1)
+            result = keep.tile([P, J], F32, name="result%d" % c)
+            for j0 in range(0, J, HALF):
+                js = slice(j0, j0 + HALF)
+                acc = bank(1)
+                for a in range(KP):
+                    nc.tensor.matmul_mx(
+                        acc[:],
+                        lhsT=wb[:, a, cols].bitcast(FP8X4),
+                        lhsT_scale=wb_bytes[4 * a : P, cols],
+                        rhs=v_words(a, j0, HALF).bitcast(FP8X4),
+                        rhs_scale=v_plane(a, j0, HALF),
+                        start=(a == 0),
+                        stop=False,
+                    )
+                for g in range(RP):
+                    nc.tensor.matmul_mx(
+                        acc[:],
+                        lhsT=up_words[:, c, g, :].bitcast(FP8X4),
+                        lhsT_scale=up_plane[:, c, g, :],
+                        rhs=h_words[:, g, js].bitcast(FP8X4),
+                        rhs_scale=h_plane[:, g, js],
+                        start=False,
+                        stop=(g == RP - 1),
+                    )
+                factor = ring.tile([P, HALF], F32, name="factor")
+                nc.scalar.activation(factor[:], acc[:], ACT.Identity, bias=bias1[:, c : c + 1])
+                nc.vector.tensor_tensor(result[:, js], listed(x0[c][:], j0, HALF), factor[:], MULT)
+                if c == NT - 1:
+                    nc.sync.dma_start(out[cols, js], result[:, js])
+            if c < NT - 1:
+                nc.sync.dma_start(out[cols, :], result[:])

@@ -42,7 +42,8 @@ def tile_list_xcross_relu_kernel(
             return psum.tile([P, HALF], F32, name="bank%d" % side)
 
         offsets = keep.tile([P, J // 16], U16, name="offsets")
-        tab_plane = held([P, KP, T // 4], I32, "tab_plane")
+        tab_plane = held([P, T // 4], I32, "tab_plane")
+        v_moved = held([P, KP - 1, J // 4], I32, "v_moved")
         dn_plane_raw = held([P, KP, R // 4], I32, "dn_plane_raw")
         wb_plane = held([P, N // 4], I32, "wb_plane")
         b_rows = held([P, P], F32, "b_rows")
@@ -56,45 +57,48 @@ def tile_list_xcross_relu_kernel(
         def load_table(a):
             nc.sync.dma_start(tab_win[a][:], tab_words[a].rearrange("p t i -> p (t i)").bitcast(I32))
 
-        def load_wb_plane(q):
-            nc.sync.dma_start(
-                wb_plane[32 * q : 32 * q + 4 * KP, :], wb_scales[:, 4 * q : 4 * q + 4, :].bitcast(I32)
-            )
-
-        tab_flat = tab_plane[:].rearrange("p a w -> p (a w)")
-        nc.gpsimd.memset(wb_plane[:], 0)
-        nc.vector.memset(tab_flat[:, 0:768], 0)
-        nc.gpsimd.memset(tab_flat[:, 768:1536], 0)
+        nc.gpsimd.dma_start(b_rows[:], b.rearrange("(c p) -> c p", p=P).unsqueeze(0).broadcast_to([P // NT, NT, P]))
         nc.vector.memset(dn_plane_raw[:], 0)
+        nc.gpsimd.memset(v_moved[:], 0)
+        nc.gpsimd.memset(wb_plane[:], 0)
         make_identity(nc, ident[:])
         nc.sync.dma_start(offsets[:], offs)
+        scale_rows = tab_scales.rearrange("a q t -> (a q) t").bitcast(I32)
+        for q in range(3):
+            nc.sync.dma_start(tab_plane[32 * q : 32 * q + 32, :], scale_rows[4 * q : 4 * q + 32, :])
+        nc.sync.dma_start(tab_plane[96:112, :], scale_rows[12:28, :])
+        nc.sync.dma_start(tab_plane[112:128, :], scale_rows[32:48, :])
         nc.sync.dma_start(dn_raw01[:], dn_words[0:2].rearrange("a p w -> p a w").bitcast(I32))
-        nc.sync.dma_start(b_rows[:], b.rearrange("(c p) -> c p", p=P).unsqueeze(0).broadcast_to([P // NT, NT, P]))
-        load_wb_plane(0)
-        for q in range(4):
-            nc.sync.dma_start(
-                tab_plane[32 * q : 32 * q + 4],
-                tab_scales[:, 4 * q : 4 * q + 4, :].rearrange("a r t -> r a t").bitcast(I32),
-            )
         load_table(0)
-        for q in range(4):
+        for r in range(4):
             nc.sync.dma_start(
-                dn_plane_raw[32 * q : 32 * q + 4],
-                dn_scales[:, 4 * q : 4 * q + 4, :].rearrange("a r n -> r a n").bitcast(I32),
+                dn_plane_raw[r:P:32], dn_scales.rearrange("a (q r) n -> r q a n", r=4)[r].bitcast(I32)
             )
         for a in range(1, KP):
             load_table(a)
         nc.sync.dma_start(dn_raw2[:], dn_words[2].bitcast(I32))
-        for q in range(1, 4):
-            load_wb_plane(q)
+
+        def listed(window, j0, width):
+            return window.indirect(offsets[:, j0 // 16 : (j0 + width) // 16])
+
+        v_rows = held([P, J], U8, "v_rows")
+        nc.vector.tensor_copy(v_rows[:], listed(tab_plane[:].bitcast(U8), 0, J))
+        for a in range(1, KP):
+            for q in range(4):
+                src = 112 + 4 * q if a == 2 else (28 if q == 3 else 32 * q + 16)
+                nc.scalar.dma_start(v_moved[32 * q : 32 * q + 4, a - 1, :], v_rows[src : src + 4, :].bitcast(I32))
+        for q in range(4):
+            nc.gpsimd.dma_start(
+                wb_plane[32 * q : 32 * q + 4 * KP, :], wb_scales[:, 4 * q : 4 * q + 4, :].bitcast(I32)
+            )
         wb = held([P, KP, N], I32, "wb")
         for a in range(KP):
             nc.sync.dma_start(wb[:, a, :], wb_words[a].rearrange("p n i -> p (n i)").bitcast(I32))
         up_raw = held([P, RP, 4, N], F32, "up_raw")
-        up_rows = upw.rearrange("(g q t i) n -> g t q i n", g=RP, q=16, t=4, i=8)
-        for g in range(RP):
-            for t in range(4):
-                nc.sync.dma_start(up_raw[:, g, t, :], up_rows[g, t])
+        up_rows = upw.rearrange("(g p t) n -> g p t n", g=RP, t=4)
+        for n0 in range(0, N, HALF):
+            for g in range(RP):
+                nc.sync.dma_start(up_raw[:, g, :, n0 : n0 + HALF], up_rows[g][:, :, n0 : n0 + HALF])
         x0 = []
         for c in range(NT):
             win = wide.tile([P, T], F32, name="window", align_bytes=64)
@@ -111,32 +115,28 @@ def tile_list_xcross_relu_kernel(
         v_half = []
 
         def new_half(name):
-            v_half.append(held([P, KP * (HALF + HALF // 4)], U32, name))
+            v_half.append(held([P, KP * HALF], U32, name))
 
         def v_words(a, j0, width):
             at = a * HALF + j0 % HALF
             return v_half[j0 // HALF][:, at : at + width]
 
         def v_plane(a, j0, width):
-            at = a * HALF + j0 % HALF
-            return v_half[j0 // HALF][:, KP * HALF :].bitcast(U8)[:, at : at + width]
+            plane = v_rows[:] if a == 0 else v_moved[:, a - 1, :].bitcast(U8)
+            return plane[:, j0 : j0 + width]
 
         def permute_dn(a):
             for g in range(RP):
                 nc.vector.tensor_copy(
-                    dn[:, a, g].rearrange("p t (q w) -> p t q w", w=4),
-                    dn_raw[a][:, 256 * g : 256 * (g + 1)].rearrange("p (q t w) -> p t q w", t=4, w=4),
+                    dn[:, a, g].bitcast(U16).rearrange("p t (c i) -> p c t i", i=8),
+                    dn_raw[a][:, 256 * g : 256 * (g + 1)].bitcast(U16).rearrange("p (c i t) -> p c t i", t=4, i=8),
                 )
                 nc.vector.tensor_copy(
-                    dn_plane[:, a, g].rearrange("p t (q w) -> p t q w", w=2),
-                    dn_plane_raw[:, a, 128 * g : 128 * (g + 1)].rearrange("p (q t w) -> p t q w", t=4, w=2),
+                    dn_plane[:, a, g].bitcast(U8).rearrange("p t (c i) -> p c t i", i=16),
+                    dn_plane_raw[:, a, 128 * g : 128 * (g + 1)].bitcast(U8).rearrange("p (c i t) -> p c t i", t=4, i=16),
                 )
 
-        def listed(window, j0, width):
-            return window.indirect(offsets[:, j0 // 16 : (j0 + width) // 16])
-
         def gather(a, j0, width):
-            nc.vector.tensor_copy(v_plane(a, j0, width), listed(tab_plane[:, a, :].bitcast(U8), j0, width))
             nc.vector.tensor_copy(v_words(a, j0, width), listed(tab_win[a][:].bitcast(U32), j0, width))
 
         def dn_pass(acc, a, g, t, j0, width):

@@ -49,9 +49,7 @@ def tile_list_xcross_relu_kernel(
         b_rows = held([P, P], F32, "b_rows")
         ident = held([P, P], F32, "ident")
 
-        dn_raw01 = held([P, KP - 1, R // 2], I32, "dn_raw01")
-        dn_raw2 = held([P, R // 2], I32, "shared")
-        dn_raw = [dn_raw01[:, 0, :], dn_raw01[:, 1, :], dn_raw2[:]]
+        dn_raw = held([P, KP, R // 2], I32, "dn_raw")
         tab_win = [wide.tile([P, T], I32, name="window", align_bytes=64) for a in range(KP)]
 
         def load_table(a):
@@ -68,15 +66,15 @@ def tile_list_xcross_relu_kernel(
             nc.sync.dma_start(tab_plane[32 * q : 32 * q + 32, :], scale_rows[4 * q : 4 * q + 32, :])
         nc.sync.dma_start(tab_plane[96:112, :], scale_rows[12:28, :])
         nc.sync.dma_start(tab_plane[112:128, :], scale_rows[32:48, :])
-        nc.sync.dma_start(dn_raw01[:], dn_words[0:2].rearrange("a p w -> p a w").bitcast(I32))
+        nc.sync.dma_start(dn_raw[:], dn_words.rearrange("a p w -> p a w").bitcast(I32))
         load_table(0)
         for r in range(4):
-            nc.sync.dma_start(
+            queue = nc.sync if r < 2 else nc.scalar
+            queue.dma_start(
                 dn_plane_raw[r:P:32], dn_scales.rearrange("a (q r) n -> r q a n", r=4)[r].bitcast(I32)
             )
         for a in range(1, KP):
             load_table(a)
-        nc.sync.dma_start(dn_raw2[:], dn_words[2].bitcast(I32))
 
         def listed(window, j0, width):
             return window.indirect(offsets[:, j0 // 16 : (j0 + width) // 16])
@@ -92,8 +90,7 @@ def tile_list_xcross_relu_kernel(
                 wb_plane[32 * q : 32 * q + 4 * KP, :], wb_scales[:, 4 * q : 4 * q + 4, :].bitcast(I32)
             )
         wb = held([P, KP, N], I32, "wb")
-        for a in range(KP):
-            nc.sync.dma_start(wb[:, a, :], wb_words[a].rearrange("p n i -> p (n i)").bitcast(I32))
+        nc.sync.dma_start(wb[:], wb_words.rearrange("a p n i -> p a (n i)").bitcast(I32))
         up_raw = held([P, RP, 4, N], F32, "up_raw")
         up_rows = upw.rearrange("(g p t) n -> g p t n", g=RP, t=4)
         for n0 in range(0, N, HALF):
@@ -129,7 +126,7 @@ def tile_list_xcross_relu_kernel(
             for g in range(RP):
                 nc.vector.tensor_copy(
                     dn[:, a, g].bitcast(U16).rearrange("p t (c i) -> p c t i", i=8),
-                    dn_raw[a][:, 256 * g : 256 * (g + 1)].bitcast(U16).rearrange("p (c i t) -> p c t i", t=4, i=8),
+                    dn_raw[:, a, 256 * g : 256 * (g + 1)].bitcast(U16).rearrange("p (c i t) -> p c t i", t=4, i=8),
                 )
                 nc.vector.tensor_copy(
                     dn_plane[:, a, g].bitcast(U8).rearrange("p t (c i) -> p c t i", i=16),
@@ -170,7 +167,7 @@ def tile_list_xcross_relu_kernel(
                 nc.scalar.activation(h_flat[g][:, t, :], first[g][t][:], ACT.Relu)
 
         late = []
-        new_half("shared")
+        new_half("v_second")
         for j0 in range(HALF, J, QUART):
             for a in range(KP):
                 gather(a, j0, QUART)
@@ -203,7 +200,7 @@ def tile_list_xcross_relu_kernel(
         up_plane = held([P, NT, RP, P], U8, "up_plane")
 
         def quantise_up(c):
-            grouped = ring.tile([P, RP * P, 4], BF16, name="up_grouped", align_bytes=64)
+            grouped = ring.tile([P, RP * P, 4], BF16, name="stage", bufs=4, align_bytes=64)
             for g in range(RP):
                 nc.scalar.copy(
                     grouped[:, g * P : (g + 1) * P, :].rearrange("p (c i) t -> p c t i", i=4),
@@ -215,10 +212,9 @@ def tile_list_xcross_relu_kernel(
 
         wb_bytes = wb_plane[:].bitcast(U8)
         quantise_up(0)
+        quantise_up(1)
         for c in range(NT):
             cols = slice(c * P, (c + 1) * P)
-            if c + 1 < NT:
-                quantise_up(c + 1)
             result = keep.tile([P, J], F32, name="result%d" % c)
             for j0 in range(0, J, HALF):
                 js = slice(j0, j0 + HALF)
@@ -243,10 +239,19 @@ def tile_list_xcross_relu_kernel(
                         start=False,
                         stop=(g == RP - 1),
                     )
-                factor = ring.tile([P, HALF], F32, name="factor")
-                nc.scalar.activation(factor[:], acc[:], ACT.Identity, bias=bias1[:, c : c + 1])
-                nc.vector.tensor_tensor(result[:, js], listed(x0[c][:], j0, HALF), factor[:], MULT)
-                if c == NT - 1:
-                    nc.sync.dma_start(out[cols, js], result[:, js])
+                factor = ring.tile([P, HALF], F32, name="stage", bufs=4, align_bytes=64)
+                width = QUART if (c, j0) == (NT - 1, HALF) else HALF
+                for s in range(0, HALF, width):
+                    piece = slice(j0 + s, j0 + s + width)
+                    nc.scalar.activation(
+                        factor[:, s : s + width], acc[:, s : s + width], ACT.Identity, bias=bias1[:, c : c + 1]
+                    )
+                    nc.vector.tensor_tensor(
+                        result[:, piece], listed(x0[c][:], j0 + s, width), factor[:, s : s + width], MULT
+                    )
+                    if c == NT - 1:
+                        nc.sync.dma_start(out[cols, piece], result[:, piece])
             if c < NT - 1:
                 nc.sync.dma_start(out[cols, :], result[:])
+            if c + 2 < NT:
+                quantise_up(c + 2)

@@ -16,6 +16,7 @@ FP8X4 = mybir.dt.float8_e4m3fn_x4
 FP4X4 = mybir.dt.float4_e2m1fn_x4
 ACT = mybir.ActivationFunctionType
 MULT = mybir.AluOpType.mult
+ADD = mybir.AluOpType.add
 
 P = 128
 KP = K // 512
@@ -31,227 +32,245 @@ def tile_list_xcross_relu_kernel(
     nc = tc.nc
     with ExitStack() as ctx:
         keep = ctx.enter_context(tc.tile_pool(name="keep", bufs=1))
-        wide = ctx.enter_context(tc.tile_pool(name="wide", bufs=8))
-        ring = ctx.enter_context(tc.tile_pool(name="ring", bufs=3))
-        psum = ctx.enter_context(tc.psum_pool(name="psum", bufs=4))
+        wide = ctx.enter_context(tc.tile_pool(name="wide", bufs=NT))
+        ring = ctx.enter_context(tc.tile_pool(name="ring", bufs=2))
+        psum = ctx.enter_context(tc.psum_pool(name="psum", bufs=8))
 
         def held(shape, dtype, name):
             return keep.tile(shape, dtype, name=name, align_bytes=64)
 
-        def bank(side):
-            return psum.tile([P, HALF], F32, name="bank%d" % side)
+        def bank():
+            return psum.tile([P, HALF], F32, name="bank")
 
         offsets = keep.tile([P, J // 16], U16, name="offsets")
-        tab_plane = held([P, T // 4], I32, "tab_plane")
+        tab_rows = held([P, T // 4], I32, "tab_rows")
         v_moved = held([P, KP - 1, J // 4], I32, "v_moved")
-        dn_plane_raw = held([P, KP, R // 4], I32, "dn_plane_raw")
+        dn_plane = held([P, KP, R // 4], I32, "dn_plane")
         wb_plane = held([P, N // 4], I32, "wb_plane")
         b_rows = held([P, P], F32, "b_rows")
         ident = held([P, P], F32, "ident")
-
-        dn_raw = held([P, KP, R // 2], I32, "dn_raw")
+        dn_first = held([P, R // 2], I32, "dn_first")
+        dn_rest = held([P, KP - 1, R // 2], I32, "dn_rest")
+        dn = [dn_first[:]] + [dn_rest[:, a - 1] for a in range(1, KP)]
         tab_win = [wide.tile([P, T], I32, name="window", align_bytes=64) for a in range(KP)]
+
+        nc.vector.memset(dn_plane[:], 0)
+        nc.vector.memset(v_moved[:], 0)
+        nc.gpsimd.dma_start(b_rows[:], b.rearrange("(c p) -> c p", p=P).unsqueeze(0).broadcast_to([P // NT, NT, P]))
+        nc.gpsimd.memset(wb_plane[:], 0)
+        make_identity(nc, ident[:])
+        for q in range(4):
+            nc.gpsimd.dma_start(
+                wb_plane[32 * q + 4 : 32 * q + 16, :], wb_scales[:, 4 * q : 4 * q + 4, :].bitcast(I32)
+            )
+        nc.sync.dma_start(offsets[:], offs)
+        rows = tab_scales.rearrange("a q t -> (a q) t").bitcast(I32)
+        for q in range(4):
+            if q == 1:
+                nc.sync.dma_start(tab_rows[32:64, :], rows.rearrange("(u w) t -> u w t", w=12)[:, 4:12, :])
+            else:
+                nc.sync.dma_start(tab_rows[32 * q : 32 * q + 32, :], rows[4 * q : 4 * q + 32, :])
+        dn_rows = dn_scales.rearrange("a (q r) n -> r q a n", r=4)
 
         def load_table(a):
             nc.sync.dma_start(tab_win[a][:], tab_words[a].rearrange("p t i -> p (t i)").bitcast(I32))
 
-        nc.gpsimd.dma_start(b_rows[:], b.rearrange("(c p) -> c p", p=P).unsqueeze(0).broadcast_to([P // NT, NT, P]))
-        nc.vector.memset(dn_plane_raw[:], 0)
-        nc.gpsimd.memset(v_moved[:], 0)
-        nc.gpsimd.memset(wb_plane[:], 0)
-        make_identity(nc, ident[:])
-        nc.sync.dma_start(offsets[:], offs)
-        scale_rows = tab_scales.rearrange("a q t -> (a q) t").bitcast(I32)
-        for q in range(3):
-            nc.sync.dma_start(tab_plane[32 * q : 32 * q + 32, :], scale_rows[4 * q : 4 * q + 32, :])
-        nc.sync.dma_start(tab_plane[96:112, :], scale_rows[12:28, :])
-        nc.sync.dma_start(tab_plane[112:128, :], scale_rows[32:48, :])
-        nc.sync.dma_start(dn_raw[:], dn_words.rearrange("a p w -> p a w").bitcast(I32))
+        nc.sync.dma_start(dn_first[:], dn_words[0].bitcast(I32))
+        nc.sync.dma_start(dn_plane[0:P:32], dn_rows[0].bitcast(I32))
         load_table(0)
-        for r in range(4):
-            queue = nc.sync if r < 2 else nc.scalar
-            queue.dma_start(
-                dn_plane_raw[r:P:32], dn_scales.rearrange("a (q r) n -> r q a n", r=4)[r].bitcast(I32)
-            )
-        for a in range(1, KP):
-            load_table(a)
+        for r in range(1, 4):
+            nc.sync.dma_start(dn_plane[r:P:32], dn_rows[r].bitcast(I32))
+        load_table(1)
+        nc.sync.dma_start(dn_rest[:], dn_words[1:KP].rearrange("a p w -> p a w").bitcast(I32))
+        load_table(2)
 
         def listed(window, j0, width):
             return window.indirect(offsets[:, j0 // 16 : (j0 + width) // 16])
 
         v_rows = held([P, J], U8, "v_rows")
-        nc.vector.tensor_copy(v_rows[:], listed(tab_plane[:].bitcast(U8), 0, J))
+        nc.vector.tensor_copy(v_rows[:], listed(tab_rows[:].bitcast(U8), 0, J))
         for a in range(1, KP):
             for q in range(4):
-                src = 112 + 4 * q if a == 2 else (28 if q == 3 else 32 * q + 16)
+                src = 16 + 4 * q if a == 1 else (60 if q == 3 else 116 + 4 * q)
                 nc.scalar.dma_start(v_moved[32 * q : 32 * q + 4, a - 1, :], v_rows[src : src + 4, :].bitcast(I32))
-        for q in range(4):
-            nc.gpsimd.dma_start(
-                wb_plane[32 * q : 32 * q + 4 * KP, :], wb_scales[:, 4 * q : 4 * q + 4, :].bitcast(I32)
-            )
+        v_words = [[held([P, HALF], U32, "v_words%d_%d" % (s, a)) for a in range(KP)] for s in range(2)]
+
+        def gather(a, s):
+            nc.vector.tensor_copy(v_words[s][a][:], listed(tab_win[a][:].bitcast(U32), s * HALF, HALF))
+
+        def v_plane(a, s):
+            plane = v_rows[:] if a == 0 else v_moved[:, a - 1, :].bitcast(U8)
+            return plane[:, s * HALF : (s + 1) * HALF]
+
         wb = held([P, KP, N], I32, "wb")
-        nc.sync.dma_start(wb[:], wb_words.rearrange("a p n i -> p a (n i)").bitcast(I32))
-        up_raw = held([P, RP, 4, N], F32, "up_raw")
         up_rows = upw.rearrange("(g p t) n -> g p t n", g=RP, t=4)
-        for n0 in range(0, N, HALF):
-            for g in range(RP):
-                nc.sync.dma_start(up_raw[:, g, :, n0 : n0 + HALF], up_rows[g][:, :, n0 : n0 + HALF])
+        up_raw = []
         x0 = []
-        for c in range(NT):
+
+        def load_up(s):
+            raw = held([P, RP, 4, HALF], F32, "up_raw%d" % s)
+            for g in range(RP):
+                nc.sync.dma_start(raw[:, g], up_rows[g][:, :, s * HALF : (s + 1) * HALF])
+            up_raw.append(raw)
+
+        def load_x0(c):
             win = wide.tile([P, T], F32, name="window", align_bytes=64)
             nc.sync.dma_start(win[:], x0T[c * P : (c + 1) * P, :])
             x0.append(win)
 
-        b_t = bank(0)
+        load_up(0)
+        load_x0(0)
+        nc.sync.dma_start(wb[:], wb_words.rearrange("a p n i -> p a (n i)").bitcast(I32))
+        for c in range(1, 3):
+            load_x0(c)
+        load_up(1)
+        for c in range(3, NT):
+            load_x0(c)
+
+        b_t = bank()
         nc.tensor.transpose(b_t[:, 0:P], b_rows[:], ident[:])
         bias1 = held([P, NT], F32, "bias1")
         nc.scalar.activation(bias1[:], b_t[:, 0:NT], ACT.Identity, bias=1.0)
 
-        dn = held([P, KP, RP, 4, 64], I32, "dn")
-        dn_plane = held([P, KP, RP, 4, 32], I32, "dn_plane")
-        v_half = []
-
-        def new_half(name):
-            v_half.append(held([P, KP * HALF], U32, name))
-
-        def v_words(a, j0, width):
-            at = a * HALF + j0 % HALF
-            return v_half[j0 // HALF][:, at : at + width]
-
-        def v_plane(a, j0, width):
-            plane = v_rows[:] if a == 0 else v_moved[:, a - 1, :].bitcast(U8)
-            return plane[:, j0 : j0 + width]
-
-        def permute_dn(a):
-            for g in range(RP):
-                nc.vector.tensor_copy(
-                    dn[:, a, g].bitcast(U16).rearrange("p t (c i) -> p c t i", i=8),
-                    dn_raw[:, a, 256 * g : 256 * (g + 1)].bitcast(U16).rearrange("p (c i t) -> p c t i", t=4, i=8),
-                )
-                nc.vector.tensor_copy(
-                    dn_plane[:, a, g].bitcast(U8).rearrange("p t (c i) -> p c t i", i=16),
-                    dn_plane_raw[:, a, 128 * g : 128 * (g + 1)].bitcast(U8).rearrange("p (c i t) -> p c t i", t=4, i=16),
-                )
-
-        def gather(a, j0, width):
-            nc.vector.tensor_copy(v_words(a, j0, width), listed(tab_win[a][:].bitcast(U32), j0, width))
-
-        def dn_pass(acc, a, g, t, j0, width):
+        def dn_pass(acc, a, g, s, u):
+            js = slice(u * P, (u + 1) * P)
             nc.tensor.matmul_mx(
-                acc,
-                lhsT=dn[:, a, g, t, :].bitcast(FP4X4),
-                lhsT_scale=dn_plane[:, a, g, t, :].bitcast(U8),
-                rhs=v_words(a, j0, width).bitcast(FP8X4),
-                rhs_scale=v_plane(a, j0, width),
+                acc[:],
+                lhsT=v_words[s][a][:, js].bitcast(FP8X4),
+                lhsT_scale=v_plane(a, s)[:, js],
+                rhs=dn[a][:, g * QUART : (g + 1) * QUART].bitcast(FP4X4),
+                rhs_scale=dn_plane[:, a, g * P : (g + 1) * P].bitcast(U8),
                 start=(a == 0),
                 stop=(a == KP - 1),
             )
 
-        h_words = held([P, RP, J], U32, "h_words")
-        h_plane = held([P, RP, J], U8, "h_plane")
+        h_words = [[held([P, HALF], U32, "h_words%d_%d" % (s, g)) for g in range(RP)] for s in range(2)]
+        h_plane = [[held([P, HALF], U8, "h_plane%d_%d" % (s, g)) for g in range(RP)] for s in range(2)]
+        up_words = [held([P, RP, P], U32, "up_words%d" % c) for c in range(NT)]
+        up_plane = [held([P, RP, P], U8, "up_plane%d" % c) for c in range(NT)]
 
         def quantise(words, plane, grouped):
-            nc.vector.quantize_mx(out=words.bitcast(FP8X4), scales=plane, in_=grouped.rearrange("p c t -> p (c t)"))
-
-        first = [[bank(g) for t in range(4)] for g in range(RP)]
-        new_half("v_first")
-        for a in range(KP):
-            permute_dn(a)
-            gather(a, 0, HALF)
-            for g in range(RP):
-                for t in range(4):
-                    dn_pass(first[g][t][:], a, g, t, 0, HALF)
-        h_flat = [held([P, 4, HALF], BF16, "h_flat%d" % g) for g in range(RP)]
-        for g in range(RP):
-            for t in range(4):
-                nc.scalar.activation(h_flat[g][:, t, :], first[g][t][:], ACT.Relu)
-
-        late = []
-        new_half("v_second")
-        for j0 in range(HALF, J, QUART):
-            for a in range(KP):
-                gather(a, j0, QUART)
-            for g in range(RP):
-                grouped = ring.tile([P, QUART, 4], BF16, name="h_late", bufs=4, align_bytes=64)
-                for s in range(0, QUART, P):
-                    acc = bank(0)
-                    for t in range(4):
-                        for a in range(KP):
-                            dn_pass(acc[:, t * P : (t + 1) * P], a, g, t, j0 + s, P)
-                    nc.scalar.activation(
-                        grouped[:, s : s + P, :], acc[:].rearrange("p (t j) -> p j t", t=4), ACT.Relu
-                    )
-                late.append((g, j0, grouped))
-
-        early = []
-        for g in range(RP):
-            grouped = ring.tile([P, HALF, 4], BF16, name="h_early", bufs=2, align_bytes=64)
-            nc.vector.tensor_copy(
-                grouped[:].rearrange("p (c i) t -> p c t i", i=4),
-                h_flat[g][:].rearrange("p t (c i) -> p c t i", i=4),
-            )
-            early.append(grouped)
-        for g in range(RP):
-            quantise(h_words[:, g, 0:HALF], h_plane[:, g, 0:HALF], early[g][:])
-        for g, j0, grouped in late:
-            quantise(h_words[:, g, j0 : j0 + QUART], h_plane[:, g, j0 : j0 + QUART], grouped[:])
-
-        up_words = held([P, NT, RP, P], U32, "up_words")
-        up_plane = held([P, NT, RP, P], U8, "up_plane")
+            nc.vector.quantize_mx(out=words.bitcast(FP8X4), scales=plane, in_=grouped)
 
         def quantise_up(c):
-            grouped = ring.tile([P, RP * P, 4], BF16, name="stage", bufs=4, align_bytes=64)
-            for g in range(RP):
-                nc.scalar.copy(
-                    grouped[:, g * P : (g + 1) * P, :].rearrange("p (c i) t -> p c t i", i=4),
-                    up_raw[:, g, :, c * P : (c + 1) * P].rearrange("p t (c i) -> p c t i", i=4),
-                )
+            if c < NT // 2:
+                grouped = ring.tile([P, RP * P, 4], BF16, name="up_stage", bufs=2, align_bytes=64)
+            else:
+                grouped = held([P, RP * P, 4], BF16, "up_words%d" % (c - 2))
+            n0 = c * P % HALF
+            copy = nc.vector.tensor_copy if c < 4 else nc.scalar.copy
+            copy(
+                grouped[:].rearrange("p (g c i) t -> p g c t i", g=RP, i=4),
+                up_raw[c * P // HALF][:, :, :, n0 : n0 + P].rearrange("p g t (c i) -> p g c t i", i=4),
+            )
             quantise(
-                up_words[:, c].rearrange("p g m -> p (g m)"), up_plane[:, c].rearrange("p g m -> p (g m)"), grouped[:]
+                up_words[c][:].rearrange("p g m -> p (g m)"),
+                up_plane[c][:].rearrange("p g m -> p (g m)"),
+                grouped[:].rearrange("p c t -> p (c t)"),
             )
 
-        wb_bytes = wb_plane[:].bitcast(U8)
-        quantise_up(0)
-        quantise_up(1)
-        for c in range(NT):
-            cols = slice(c * P, (c + 1) * P)
-            result = keep.tile([P, J], F32, name="result%d" % c)
-            for j0 in range(0, J, HALF):
-                js = slice(j0, j0 + HALF)
-                acc = bank(1)
+        def relu(acc):
+            flat = ring.tile([P, HALF], BF16, name="flat", bufs=12, align_bytes=64)
+            nc.scalar.activation(
+                flat[:].rearrange("j (w p e) -> j w p e", w=2, e=2),
+                acc[:].rearrange("j (p w e) -> j w p e", w=2, e=2),
+                ACT.Relu,
+            )
+            return flat
+
+        def turn(s, g, flats):
+            grouped = ring.tile([P, HALF, 2], F32, name="grouped", bufs=2, align_bytes=64)
+            for pair in range(2):
+                turned = bank()
+                for k in range(2):
+                    for w in range(2):
+                        at = (2 * k + w) * P
+                        words = flats[2 * pair + k][:].bitcast(F32)
+                        nc.tensor.transpose(turned[:, at : at + P], words[:, w * P : (w + 1) * P], ident[:])
+                nc.scalar.copy(
+                    grouped[:, pair * QUART : (pair + 1) * QUART, :].rearrange("p (k j) w -> p k j w", k=2),
+                    turned[:].rearrange("p (k w j) -> p k j w", k=2, w=2),
+                )
+            quantise(h_words[s][g][:], h_plane[s][g][:], grouped[:].rearrange("p j w -> p (j w)").bitcast(BF16))
+
+        first = [[bank() for u in range(4)] for g in range(RP)]
+        for a in range(KP):
+            gather(a, 0)
+            for g in range(RP):
+                for u in range(4):
+                    dn_pass(first[g][u], a, g, 0, u)
+        for a in range(KP):
+            gather(a, 1)
+        flats = [[[relu(acc) for acc in first[g]] for g in range(RP)], []]
+        for g in range(RP):
+            made = []
+            for u in range(4):
+                acc = bank()
                 for a in range(KP):
-                    nc.tensor.matmul_mx(
-                        acc[:],
-                        lhsT=wb[:, a, cols].bitcast(FP8X4),
-                        lhsT_scale=wb_bytes[4 * a : P, cols],
-                        rhs=v_words(a, j0, HALF).bitcast(FP8X4),
-                        rhs_scale=v_plane(a, j0, HALF),
-                        start=(a == 0),
-                        stop=False,
-                    )
+                    dn_pass(acc, a, g, 1, u)
+                made.append(acc)
+            if g == 0:
+                for gg in range(RP):
+                    turn(0, gg, flats[0][gg])
+            flats[1].append([relu(acc) for acc in made])
+        for c in range(NT // 2):
+            quantise_up(c)
+        picked = {}
+        whole = held([P, J], F32, "picked0")
+        nc.vector.tensor_copy(whole[:], listed(x0[0][:], 0, J))
+        picked[0, 0], picked[0, 1] = whole[:, 0:HALF], whole[:, HALF:J]
+        for c, name in ((1, "dn_first"),):
+            tile = held([P, HALF], F32, name)
+            nc.vector.tensor_copy(tile[:], listed(x0[c][:], HALF, HALF))
+            picked[c, 1] = tile[:]
+        result = [held([P, J], F32, "result%d" % c)[:] for c in range(NT)]
+        order = [(c, 0) for c in range(4)] + [(2, 1), (3, 1)] + [(c, s) for c in range(4, NT) for s in range(2)] + [(0, 1), (1, 1)]
+        ready = NT // 2
+        for step, (c, s) in enumerate(order):
+            if step == 2:
                 for g in range(RP):
-                    nc.tensor.matmul_mx(
-                        acc[:],
-                        lhsT=up_words[:, c, g, :].bitcast(FP8X4),
-                        lhsT_scale=up_plane[:, c, g, :],
-                        rhs=h_words[:, g, js].bitcast(FP8X4),
-                        rhs_scale=h_plane[:, g, js],
-                        start=False,
-                        stop=(g == RP - 1),
+                    turn(1, g, flats[1][g])
+            while ready < min(NT, max(cc for cc, ss in order[: step + 3]) + 1):
+                quantise_up(ready)
+                ready = ready + 1
+            cols = slice(c * P, (c + 1) * P)
+            acc = bank()
+            for a in range(KP):
+                nc.tensor.matmul_mx(
+                    acc[:],
+                    lhsT=wb[:, a, cols].bitcast(FP8X4),
+                    lhsT_scale=wb_plane[4 * a + 4 : P, :].bitcast(U8)[:, cols],
+                    rhs=v_words[s][a][:].bitcast(FP8X4),
+                    rhs_scale=v_plane(a, s),
+                    start=(a == 0),
+                    stop=False,
+                )
+            for g in range(RP):
+                nc.tensor.matmul_mx(
+                    acc[:],
+                    lhsT=up_words[c][:, g, :].bitcast(FP8X4),
+                    lhsT_scale=up_plane[c][:, g, :],
+                    rhs=h_words[s][g][:].bitcast(FP8X4),
+                    rhs_scale=h_plane[s][g][:],
+                    start=False,
+                    stop=(g == RP - 1),
+                )
+            if (c, s) not in picked:
+                factor = ring.tile([P, HALF], F32, name="factor", bufs=5, align_bytes=64)
+            width = QUART if step == len(order) - 1 else HALF
+            for j in range(0, HALF, width):
+                piece = slice(s * HALF + j, s * HALF + j + width)
+                part = slice(j, j + width)
+                if (c, s) in picked:
+                    nc.vector.scalar_tensor_tensor(
+                        result[c][:, piece], acc[:, part], bias1[:, c : c + 1], picked[c, s][:, part], ADD, MULT
                     )
-                factor = ring.tile([P, HALF], F32, name="stage", bufs=4, align_bytes=64)
-                width = QUART if (c, j0) == (NT - 1, HALF) else HALF
-                for s in range(0, HALF, width):
-                    piece = slice(j0 + s, j0 + s + width)
-                    nc.scalar.activation(
-                        factor[:, s : s + width], acc[:, s : s + width], ACT.Identity, bias=bias1[:, c : c + 1]
-                    )
+                else:
+                    nc.scalar.activation(factor[:, part], acc[:, part], ACT.Identity, bias=bias1[:, c : c + 1])
                     nc.vector.tensor_tensor(
-                        result[:, piece], listed(x0[c][:], j0 + s, width), factor[:, s : s + width], MULT
+                        result[c][:, piece], listed(x0[c][:], s * HALF + j, width), factor[:, part], MULT
                     )
-                    if c == NT - 1:
-                        nc.sync.dma_start(out[cols, piece], result[:, piece])
-            if c < NT - 1:
-                nc.sync.dma_start(out[cols, :], result[:])
-            if c + 2 < NT:
-                quantise_up(c + 2)
+                if c < 2:
+                    nc.sync.dma_start(out[cols, piece], result[c][:, piece])
+            if c >= 2 and s == 1:
+                nc.sync.dma_start(out[cols, :], result[c])

@@ -92,7 +92,8 @@ def tile_list_xcross_relu_kernel(
         for a in range(1, KP):
             for q in range(4):
                 src = 16 + 4 * q if a == 1 else (60 if q == 3 else 116 + 4 * q)
-                nc.scalar.dma_start(v_moved[32 * q : 32 * q + 4, a - 1, :], v_rows[src : src + 4, :].bitcast(I32))
+                queue = nc.scalar if a == 1 else nc.gpsimd
+                queue.dma_start(v_moved[32 * q : 32 * q + 4, a - 1, :], v_rows[src : src + 4, :].bitcast(I32))
         v_words = [[held([P, HALF], U32, "v_words%d_%d" % (s, a)) for a in range(KP)] for s in range(2)]
 
         def gather(a, s):

@@ -24,6 +24,8 @@ RP = R // 512
 NT = N // P
 HALF = 512
 QUART = 256
+LATE_X0 = 5
+LATE_WORDS = T + R // 2 + KP * N + RP * 4 * N + LATE_X0 * T
 
 
 def tile_list_xcross_relu_kernel(
@@ -32,7 +34,6 @@ def tile_list_xcross_relu_kernel(
     nc = tc.nc
     with ExitStack() as ctx:
         keep = ctx.enter_context(tc.tile_pool(name="keep", bufs=1))
-        wide = ctx.enter_context(tc.tile_pool(name="wide", bufs=NT))
         ring = ctx.enter_context(tc.tile_pool(name="ring", bufs=2))
         psum = ctx.enter_context(tc.psum_pool(name="psum", bufs=8))
 
@@ -43,57 +44,69 @@ def tile_list_xcross_relu_kernel(
             return psum.tile([P, HALF], F32, name="bank")
 
         offsets = keep.tile([P, J // 16], U16, name="offsets")
-        tab_rows = held([P, T // 4], I32, "tab_rows")
         v_moved = held([P, KP - 1, J // 4], I32, "v_moved")
         dn_plane = held([P, KP, R // 4], I32, "dn_plane")
         wb_plane = held([P, N // 4], I32, "wb_plane")
         b_rows = held([P, P], F32, "b_rows")
         ident = held([P, P], F32, "ident")
-        dn_first = held([P, R // 2], I32, "dn_first")
-        dn_rest = held([P, KP - 1, R // 2], I32, "dn_rest")
-        dn = [dn_first[:]] + [dn_rest[:, a - 1] for a in range(1, KP)]
-        tab_win = [wide.tile([P, T], I32, name="window", align_bytes=64) for a in range(KP)]
+        dn = [held([P, R // 2], I32, "dn%d" % a) for a in range(KP - 1)]
+        tab_win = [held([P, T], I32, "window%d" % a) for a in range(KP - 1)]
+        with tc.tile_pool(name="head", bufs=1) as head_pool:
+            space = head_pool.tile([P, LATE_WORDS], I32, name="space", align_bytes=64)
+            tab_rows = space[:, 0 : T // 4]
 
-        nc.vector.memset(dn_plane[:], 0)
-        nc.vector.memset(v_moved[:], 0)
-        nc.gpsimd.dma_start(b_rows[:], b.rearrange("(c p) -> c p", p=P).unsqueeze(0).broadcast_to([P // NT, NT, P]))
-        nc.gpsimd.memset(wb_plane[:], 0)
-        make_identity(nc, ident[:])
-        for q in range(4):
-            nc.gpsimd.dma_start(
-                wb_plane[32 * q + 4 : 32 * q + 16, :], wb_scales[:, 4 * q : 4 * q + 4, :].bitcast(I32)
-            )
-        nc.sync.dma_start(offsets[:], offs)
-        rows = tab_scales.rearrange("a q t -> (a q) t").bitcast(I32)
-        for q in range(4):
-            if q == 1:
-                nc.sync.dma_start(tab_rows[32:64, :], rows.rearrange("(u w) t -> u w t", w=12)[:, 4:12, :])
-            else:
-                nc.sync.dma_start(tab_rows[32 * q : 32 * q + 32, :], rows[4 * q : 4 * q + 32, :])
-        dn_rows = dn_scales.rearrange("a (q r) n -> r q a n", r=4)
-
-        def load_table(a):
-            nc.sync.dma_start(tab_win[a][:], tab_words[a].rearrange("p t i -> p (t i)").bitcast(I32))
-
-        nc.sync.dma_start(dn_first[:], dn_words[0].bitcast(I32))
-        nc.sync.dma_start(dn_plane[0:P:32], dn_rows[0].bitcast(I32))
-        load_table(0)
-        for r in range(1, 4):
-            nc.sync.dma_start(dn_plane[r:P:32], dn_rows[r].bitcast(I32))
-        load_table(1)
-        nc.sync.dma_start(dn_rest[:], dn_words[1:KP].rearrange("a p w -> p a w").bitcast(I32))
-        load_table(2)
-
-        def listed(window, j0, width):
-            return window.indirect(offsets[:, j0 // 16 : (j0 + width) // 16])
-
-        v_rows = held([P, J], U8, "v_rows")
-        nc.vector.tensor_copy(v_rows[:], listed(tab_rows[:].bitcast(U8), 0, J))
-        for a in range(1, KP):
+            nc.vector.memset(dn_plane[:], 0)
+            nc.vector.memset(v_moved[:], 0)
+            nc.gpsimd.memset(b_rows[:], 0.0)
+            nc.gpsimd.dma_start(b_rows[0:NT, :], b.rearrange("(c p) -> c p", p=P))
+            nc.gpsimd.memset(wb_plane[:], 0)
+            make_identity(nc, ident[:])
             for q in range(4):
-                src = 16 + 4 * q if a == 1 else (60 if q == 3 else 116 + 4 * q)
-                queue = nc.scalar if a == 1 else nc.gpsimd
-                queue.dma_start(v_moved[32 * q : 32 * q + 4, a - 1, :], v_rows[src : src + 4, :].bitcast(I32))
+                nc.gpsimd.dma_start(
+                    wb_plane[32 * q + 4 : 32 * q + 16, :], wb_scales[:, 4 * q : 4 * q + 4, :].bitcast(I32)
+                )
+            nc.sync.dma_start(offsets[:], offs)
+            rows = tab_scales.rearrange("a q t -> (a q) t").bitcast(I32)
+            for q in range(3):
+                nc.sync.dma_start(tab_rows[32 * q : 32 * q + 32, :], rows[4 * q : 4 * q + 32, :])
+            nc.sync.dma_start(tab_rows[96:112, :], rows[12:28, :])
+            nc.sync.dma_start(tab_rows[112:128, :], rows[32:48, :])
+            dn_rows = dn_scales.rearrange("a (q r) n -> r q a n", r=4)
+
+            def load_table(a):
+                nc.sync.dma_start(tab_win[a][:], tab_words[a].rearrange("p t i -> p (t i)").bitcast(I32))
+
+            def load_dn(a):
+                nc.sync.dma_start(dn[a][:], dn_words[a].bitcast(I32))
+
+            load_table(0)
+            load_dn(0)
+            for r in range(4):
+                nc.sync.dma_start(dn_plane[r:P:32], dn_rows[r].bitcast(I32))
+            load_table(1)
+            load_dn(1)
+
+            def listed(window, j0, width):
+                return window.indirect(offsets[:, j0 // 16 : (j0 + width) // 16])
+
+            v_rows = held([P, J], U8, "v_rows")
+            nc.vector.tensor_copy(v_rows[:], listed(tab_rows.bitcast(U8), 0, J))
+        late = ctx.enter_context(tc.tile_pool(name="late", bufs=1))
+
+        def late_tile(shape, dtype, name):
+            return late.tile(shape, dtype, name=name, align_bytes=64)
+
+        def move_rows(a):
+            for q in range(4):
+                src = 16 + 4 * q if a == 1 else 112 + 4 * q
+                nc.sync.dma_start(v_moved[32 * q : 32 * q + 4, a - 1, :], v_rows[src : src + 4, :].bitcast(I32))
+
+        tab_win.append(late_tile([P, T], I32, "window2"))
+        dn.append(late_tile([P, R // 2], I32, "dn2"))
+        move_rows(1)
+        load_table(2)
+        load_dn(2)
+        move_rows(2)
         v_words = [[held([P, HALF], U32, "v_words%d_%d" % (s, a)) for a in range(KP)] for s in range(2)]
 
         def gather(a, s):
@@ -103,29 +116,34 @@ def tile_list_xcross_relu_kernel(
             plane = v_rows[:] if a == 0 else v_moved[:, a - 1, :].bitcast(U8)
             return plane[:, s * HALF : (s + 1) * HALF]
 
-        wb = held([P, KP, N], I32, "wb")
+        wb = late_tile([P, KP, N], I32, "wb")
         up_rows = upw.rearrange("(g p t) n -> g p t n", g=RP, t=4)
         up_raw = []
         x0 = []
 
         def load_up(s):
-            raw = held([P, RP, 4, HALF], F32, "up_raw%d" % s)
+            raw = late_tile([P, RP, 4, HALF], F32, "up_raw%d" % s)
             for g in range(RP):
                 nc.sync.dma_start(raw[:, g], up_rows[g][:, :, s * HALF : (s + 1) * HALF])
             up_raw.append(raw)
 
         def load_x0(c):
-            win = wide.tile([P, T], F32, name="window", align_bytes=64)
+            if c < LATE_X0:
+                win = late_tile([P, T], F32, "x0_%d" % c)
+            elif c < NT - 1:
+                win = held([P, T], F32, "window%d" % (c - LATE_X0))
+            else:
+                win = late_tile([P, T], F32, "window2")
             nc.sync.dma_start(win[:], x0T[c * P : (c + 1) * P, :])
             x0.append(win)
 
-        load_up(0)
         load_x0(0)
+        load_up(0)
         nc.sync.dma_start(wb[:], wb_words.rearrange("a p n i -> p a (n i)").bitcast(I32))
-        for c in range(1, 3):
+        for c in range(1, 4):
             load_x0(c)
         load_up(1)
-        for c in range(3, NT):
+        for c in range(4, LATE_X0):
             load_x0(c)
 
         b_t = bank()
@@ -154,8 +172,10 @@ def tile_list_xcross_relu_kernel(
             nc.vector.quantize_mx(out=words.bitcast(FP8X4), scales=plane, in_=grouped)
 
         def quantise_up(c):
-            if c < NT // 2:
+            if c < 2:
                 grouped = ring.tile([P, RP * P, 4], BF16, name="up_stage", bufs=2, align_bytes=64)
+            elif c < NT // 2:
+                grouped = ring.tile([P, RP * P, 4], BF16, name="grouped", bufs=2, align_bytes=64)
             else:
                 grouped = held([P, RP * P, 4], BF16, "up_words%d" % (c - 2))
             n0 = c * P % HALF
@@ -202,6 +222,13 @@ def tile_list_xcross_relu_kernel(
                     dn_pass(first[g][u], a, g, 0, u)
         for a in range(KP):
             gather(a, 1)
+        for c in range(LATE_X0, NT):
+            load_x0(c)
+        whole = held([P, J], F32, "picked0")
+        nc.vector.tensor_copy(whole[:], listed(x0[0][:], 0, J))
+        picked = {(0, 0): whole[:, 0:HALF], (0, 1): whole[:, HALF:J]}
+        for c in range(2):
+            quantise_up(c)
         flats = [[[relu(acc) for acc in first[g]] for g in range(RP)], []]
         for g in range(RP):
             made = []
@@ -214,18 +241,10 @@ def tile_list_xcross_relu_kernel(
                 for gg in range(RP):
                     turn(0, gg, flats[0][gg])
             flats[1].append([relu(acc) for acc in made])
-        for c in range(NT // 2):
+        for c in range(2, NT // 2):
             quantise_up(c)
-        picked = {}
-        whole = held([P, J], F32, "picked0")
-        nc.vector.tensor_copy(whole[:], listed(x0[0][:], 0, J))
-        picked[0, 0], picked[0, 1] = whole[:, 0:HALF], whole[:, HALF:J]
-        for c, name in ((1, "dn_first"),):
-            tile = held([P, HALF], F32, name)
-            nc.vector.tensor_copy(tile[:], listed(x0[c][:], HALF, HALF))
-            picked[c, 1] = tile[:]
-        result = [held([P, J], F32, "result%d" % c)[:] for c in range(NT)]
-        order = [(c, 0) for c in range(4)] + [(2, 1), (3, 1)] + [(c, s) for c in range(4, NT) for s in range(2)] + [(0, 1), (1, 1)]
+        result = [held([P, J], F32, "result%d" % c) for c in range(NT)]
+        order = [(c, 0) for c in range(4)] + [(1, 1), (2, 1), (3, 1), (0, 1)] + [(c, s) for c in range(4, NT) for s in range(2)]
         ready = NT // 2
         for step, (c, s) in enumerate(order):
             if step == 2:
@@ -271,7 +290,7 @@ def tile_list_xcross_relu_kernel(
                     nc.vector.tensor_tensor(
                         result[c][:, piece], listed(x0[c][:], s * HALF + j, width), factor[:, part], MULT
                     )
-                if c < 2:
+                if c == NT - 1:
                     nc.sync.dma_start(out[cols, piece], result[c][:, piece])
-            if c >= 2 and s == 1:
-                nc.sync.dma_start(out[cols, :], result[c])
+            if c < NT - 1 and s == 1:
+                nc.sync.dma_start(out[cols, :], result[c][:])

@@ -17,6 +17,7 @@ FP4X4 = mybir.dt.float4_e2m1fn_x4
 ACT = mybir.ActivationFunctionType
 MULT = mybir.AluOpType.mult
 ADD = mybir.AluOpType.add
+MAX = mybir.AluOpType.max
 
 P = 128
 KP = K // 512
@@ -97,9 +98,11 @@ def tile_list_xcross_relu_kernel(
             return late.tile(shape, dtype, name=name, align_bytes=64)
 
         def move_rows(a):
-            for q in range(4):
-                src = 16 + 4 * q if a == 1 else 112 + 4 * q
-                nc.sync.dma_start(v_moved[32 * q : 32 * q + 4, a - 1, :], v_rows[src : src + 4, :].bitcast(I32))
+            first_row = 16 if a == 1 else 112
+            for r in range(4):
+                nc.sync.dma_start(
+                    v_moved[r:P:32, a - 1, :], v_rows[first_row + r : first_row + 16 : 4, :].bitcast(I32)
+                )
 
         tab_win.append(late_tile([P, T], I32, "window2"))
         dn.append(late_tile([P, R // 2], I32, "dn2"))
@@ -109,22 +112,24 @@ def tile_list_xcross_relu_kernel(
         move_rows(2)
         v_words = [[held([P, HALF], U32, "v_words%d_%d" % (s, a)) for a in range(KP)] for s in range(2)]
 
-        def gather(a, s):
-            nc.vector.tensor_copy(v_words[s][a][:], listed(tab_win[a][:].bitcast(U32), s * HALF, HALF))
+        def gather(a, s, width=HALF):
+            for j in range(0, HALF, width):
+                nc.vector.tensor_copy(
+                    v_words[s][a][:, j : j + width], listed(tab_win[a][:].bitcast(U32), s * HALF + j, width)
+                )
 
         def v_plane(a, s):
             plane = v_rows[:] if a == 0 else v_moved[:, a - 1, :].bitcast(U8)
             return plane[:, s * HALF : (s + 1) * HALF]
 
         wb = late_tile([P, KP, N], I32, "wb")
-        up_rows = upw.rearrange("(g p t) n -> g p t n", g=RP, t=4)
+        up_rows = upw.rearrange("(g p t) n -> g p (t n)", g=RP, t=4)
         up_raw = []
         x0 = []
 
-        def load_up(s):
-            raw = late_tile([P, RP, 4, HALF], F32, "up_raw%d" % s)
-            for g in range(RP):
-                nc.sync.dma_start(raw[:, g], up_rows[g][:, :, s * HALF : (s + 1) * HALF])
+        def load_up(g):
+            raw = late_tile([P, 4 * N], F32, "up_raw%d" % g)
+            nc.sync.dma_start(raw[:], up_rows[g])
             up_raw.append(raw)
 
         def load_x0(c):
@@ -137,13 +142,10 @@ def tile_list_xcross_relu_kernel(
             nc.sync.dma_start(win[:], x0T[c * P : (c + 1) * P, :])
             x0.append(win)
 
-        load_x0(0)
-        load_up(0)
+        for g in range(RP):
+            load_up(g)
         nc.sync.dma_start(wb[:], wb_words.rearrange("a p n i -> p a (n i)").bitcast(I32))
-        for c in range(1, 4):
-            load_x0(c)
-        load_up(1)
-        for c in range(4, LATE_X0):
+        for c in range(LATE_X0):
             load_x0(c)
 
         b_t = bank()
@@ -165,42 +167,34 @@ def tile_list_xcross_relu_kernel(
 
         h_words = [[held([P, HALF], U32, "h_words%d_%d" % (s, g)) for g in range(RP)] for s in range(2)]
         h_plane = [[held([P, HALF], U8, "h_plane%d_%d" % (s, g)) for g in range(RP)] for s in range(2)]
-        up_words = [held([P, RP, P], U32, "up_words%d" % c) for c in range(NT)]
-        up_plane = [held([P, RP, P], U8, "up_plane%d" % c) for c in range(NT)]
+        up_words = [[held([P, QUART], U32, "up_words%d_%d" % (g, k)) for k in range(4)] for g in range(RP)]
+        up_plane = [[held([P, QUART], U8, "up_plane%d_%d" % (g, k)) for k in range(4)] for g in range(RP)]
 
         def quantise(words, plane, grouped):
             nc.vector.quantize_mx(out=words.bitcast(FP8X4), scales=plane, in_=grouped)
 
-        def quantise_up(c):
-            if c < 2:
-                grouped = ring.tile([P, RP * P, 4], BF16, name="up_stage", bufs=2, align_bytes=64)
-            elif c < NT // 2:
-                grouped = ring.tile([P, RP * P, 4], BF16, name="grouped", bufs=2, align_bytes=64)
-            else:
-                grouped = held([P, RP * P, 4], BF16, "up_words%d" % (c - 2))
-            n0 = c * P % HALF
-            copy = nc.vector.tensor_copy if c < 4 else nc.scalar.copy
-            copy(
-                grouped[:].rearrange("p (g c i) t -> p g c t i", g=RP, i=4),
-                up_raw[c * P // HALF][:, :, :, n0 : n0 + P].rearrange("p g t (c i) -> p g c t i", i=4),
-            )
-            quantise(
-                up_words[c][:].rearrange("p g m -> p (g m)"),
-                up_plane[c][:].rearrange("p g m -> p (g m)"),
-                grouped[:].rearrange("p c t -> p (c t)"),
-            )
+        def quantise_up(g, tag):
+            source = up_raw[g][:].rearrange("p (t n) -> p t n", t=4)
+            for k in range(4):
+                grouped = ring.tile([P, QUART, 4], BF16, name=tag, bufs=2, align_bytes=64)
+                nc.vector.tensor_copy(
+                    grouped[:].rearrange("p (c i) t -> p c t i", i=4),
+                    source[:, :, k * QUART : (k + 1) * QUART].rearrange("p t (c i) -> p c t i", i=4),
+                )
+                quantise(up_words[g][k][:], up_plane[g][k][:], grouped[:].rearrange("p c t -> p (c t)"))
 
-        def relu(acc):
+        def relu(acc, on_vector=False):
             flat = ring.tile([P, HALF], BF16, name="flat", bufs=12, align_bytes=64)
-            nc.scalar.activation(
-                flat[:].rearrange("j (w p e) -> j w p e", w=2, e=2),
-                acc[:].rearrange("j (p w e) -> j w p e", w=2, e=2),
-                ACT.Relu,
-            )
+            dst = flat[:].rearrange("j (w p e) -> j w p e", w=2, e=2)
+            src = acc[:].rearrange("j (p w e) -> j w p e", w=2, e=2)
+            if on_vector:
+                nc.vector.tensor_scalar(dst, src, 0.0, None, MAX)
+            else:
+                nc.scalar.activation(dst, src, ACT.Relu)
             return flat
 
         def turn(s, g, flats):
-            grouped = ring.tile([P, HALF, 2], F32, name="grouped", bufs=2, align_bytes=64)
+            grouped = ring.tile([P, HALF, 2], F32, name="stage%d" % s, bufs=2, align_bytes=64)
             for pair in range(2):
                 turned = bank()
                 for k in range(2):
@@ -216,20 +210,17 @@ def tile_list_xcross_relu_kernel(
 
         first = [[bank() for u in range(4)] for g in range(RP)]
         for a in range(KP):
-            gather(a, 0)
-            for g in range(RP):
-                for u in range(4):
-                    dn_pass(first[g][u], a, g, 0, u)
+            gather(a, 0, HALF if a == 1 else QUART)
+            for pair in range(2):
+                for g in range(RP):
+                    for u in range(2 * pair, 2 * pair + 2):
+                        dn_pass(first[g][u], a, g, 0, u)
         for a in range(KP):
             gather(a, 1)
         for c in range(LATE_X0, NT):
             load_x0(c)
-        whole = held([P, J], F32, "picked0")
-        nc.vector.tensor_copy(whole[:], listed(x0[0][:], 0, J))
-        picked = {(0, 0): whole[:, 0:HALF], (0, 1): whole[:, HALF:J]}
-        for c in range(2):
-            quantise_up(c)
-        flats = [[[relu(acc) for acc in first[g]] for g in range(RP)], []]
+        flats = [[[relu(acc, g == 1) for acc in first[g]] for g in range(RP)], []]
+        quantise_up(0, "stage1")
         for g in range(RP):
             made = []
             for u in range(4):
@@ -241,19 +232,16 @@ def tile_list_xcross_relu_kernel(
                 for gg in range(RP):
                     turn(0, gg, flats[0][gg])
             flats[1].append([relu(acc) for acc in made])
-        for c in range(2, NT // 2):
-            quantise_up(c)
-        result = [held([P, J], F32, "result%d" % c) for c in range(NT)]
-        order = [(c, 0) for c in range(4)] + [(1, 1), (2, 1), (3, 1), (0, 1)] + [(c, s) for c in range(4, NT) for s in range(2)]
-        ready = NT // 2
+        quantise_up(1, "stage0")
+        pairs = [held([P, 2, J], F32, "pair%d" % k) for k in range(NT // 2)]
+        result = [pairs[c // 2][:, c % 2] for c in range(NT)]
+        order = [(0, 0), (1, 0), (0, 1), (1, 1)] + [(c, s) for c in range(2, NT) for s in range(2)]
         for step, (c, s) in enumerate(order):
-            if step == 2:
+            if step == 0:
                 for g in range(RP):
                     turn(1, g, flats[1][g])
-            while ready < min(NT, max(cc for cc, ss in order[: step + 3]) + 1):
-                quantise_up(ready)
-                ready = ready + 1
             cols = slice(c * P, (c + 1) * P)
+            part_cols = slice(c % 2 * P, (c % 2 + 1) * P)
             acc = bank()
             for a in range(KP):
                 nc.tensor.matmul_mx(
@@ -268,29 +256,26 @@ def tile_list_xcross_relu_kernel(
             for g in range(RP):
                 nc.tensor.matmul_mx(
                     acc[:],
-                    lhsT=up_words[c][:, g, :].bitcast(FP8X4),
-                    lhsT_scale=up_plane[c][:, g, :],
+                    lhsT=up_words[g][c // 2][:, part_cols].bitcast(FP8X4),
+                    lhsT_scale=up_plane[g][c // 2][:, part_cols],
                     rhs=h_words[s][g][:].bitcast(FP8X4),
                     rhs_scale=h_plane[s][g][:],
                     start=False,
                     stop=(g == RP - 1),
                 )
-            if (c, s) not in picked:
-                factor = ring.tile([P, HALF], F32, name="factor", bufs=5, align_bytes=64)
+            factor = ring.tile([P, HALF], F32, name="factor", bufs=5, align_bytes=64)
             width = QUART if step == len(order) - 1 else HALF
             for j in range(0, HALF, width):
                 piece = slice(s * HALF + j, s * HALF + j + width)
                 part = slice(j, j + width)
-                if (c, s) in picked:
-                    nc.vector.scalar_tensor_tensor(
-                        result[c][:, piece], acc[:, part], bias1[:, c : c + 1], picked[c, s][:, part], ADD, MULT
-                    )
-                else:
-                    nc.scalar.activation(factor[:, part], acc[:, part], ACT.Identity, bias=bias1[:, c : c + 1])
-                    nc.vector.tensor_tensor(
-                        result[c][:, piece], listed(x0[c][:], s * HALF + j, width), factor[:, part], MULT
-                    )
+                nc.scalar.activation(factor[:, part], acc[:, part], ACT.Identity, bias=bias1[:, c : c + 1])
+                nc.vector.tensor_tensor(
+                    result[c][:, piece], listed(x0[c][:], s * HALF + j, width), factor[:, part], MULT
+                )
                 if c == NT - 1:
                     nc.sync.dma_start(out[cols, piece], result[c][:, piece])
-            if c < NT - 1 and s == 1:
-                nc.sync.dma_start(out[cols, :], result[c][:])
+            if c == NT - 2 and s == 1:
+                nc.sync.dma_start(out[cols, :], result[c])
+            if c in (1, 3, 5) and s == 1:
+                rows_out = out[(c - 1) * P : (c + 1) * P, :].rearrange("(k p) j -> p k j", k=2)
+                nc.sync.dma_start(rows_out, pairs[c // 2][:])

@@ -122,15 +122,22 @@ def tile_list_xcross_relu_kernel(
             plane = v_rows[:] if a == 0 else v_moved[:, a - 1, :].bitcast(U8)
             return plane[:, s * HALF : (s + 1) * HALF]
 
-        wb = late_tile([P, KP, N], I32, "wb")
-        up_rows = upw.rearrange("(g p t) n -> g p (t n)", g=RP, t=4)
+        wb = []
+        up_rows = upw.rearrange("(g p t) n -> g p t n", g=RP, t=4)
+        wb_rows = wb_words.rearrange("a p n i -> p a (n i)").bitcast(I32)
         up_raw = []
         x0 = []
 
-        def load_up(g):
-            raw = late_tile([P, 4 * N], F32, "up_raw%d" % g)
-            nc.sync.dma_start(raw[:], up_rows[g])
+        def load_up(s):
+            raw = late_tile([P, RP, 4, HALF], F32, "up_raw%d" % s)
+            for g in range(RP):
+                nc.sync.dma_start(raw[:, g], up_rows[g][:, :, s * HALF : (s + 1) * HALF])
             up_raw.append(raw)
+
+        def load_wb(s):
+            words = late_tile([P, KP, HALF], I32, "wb%d" % s)
+            nc.sync.dma_start(words[:], wb_rows[:, :, s * HALF : (s + 1) * HALF])
+            wb.append(words)
 
         def load_x0(c):
             if c < LATE_X0:
@@ -142,16 +149,16 @@ def tile_list_xcross_relu_kernel(
             nc.sync.dma_start(win[:], x0T[c * P : (c + 1) * P, :])
             x0.append(win)
 
-        for g in range(RP):
-            load_up(g)
-        nc.sync.dma_start(wb[:], wb_words.rearrange("a p n i -> p a (n i)").bitcast(I32))
-        for c in range(LATE_X0):
+        for c in range(2):
             load_x0(c)
-
-        b_t = bank()
-        nc.tensor.transpose(b_t[:, 0:P], b_rows[:], ident[:])
-        bias1 = held([P, NT], F32, "bias1")
-        nc.scalar.activation(bias1[:], b_t[:, 0:NT], ACT.Identity, bias=1.0)
+        load_up(0)
+        load_wb(0)
+        load_x0(2)
+        load_up(1)
+        load_x0(3)
+        load_wb(1)
+        for c in range(4, LATE_X0):
+            load_x0(c)
 
         def dn_pass(acc, a, g, s, u):
             js = slice(u * P, (u + 1) * P)
@@ -167,21 +174,28 @@ def tile_list_xcross_relu_kernel(
 
         h_words = [[held([P, HALF], U32, "h_words%d_%d" % (s, g)) for g in range(RP)] for s in range(2)]
         h_plane = [[held([P, HALF], U8, "h_plane%d_%d" % (s, g)) for g in range(RP)] for s in range(2)]
-        up_words = [[held([P, QUART], U32, "up_words%d_%d" % (g, k)) for k in range(4)] for g in range(RP)]
-        up_plane = [[held([P, QUART], U8, "up_plane%d_%d" % (g, k)) for k in range(4)] for g in range(RP)]
+        up_words = [held([P, RP, P], U32, "up_words%d" % c) for c in range(NT)]
+        up_plane = [held([P, RP, P], U8, "up_plane%d" % c) for c in range(NT)]
 
         def quantise(words, plane, grouped):
             nc.vector.quantize_mx(out=words.bitcast(FP8X4), scales=plane, in_=grouped)
 
-        def quantise_up(g, tag):
-            source = up_raw[g][:].rearrange("p (t n) -> p t n", t=4)
-            for k in range(4):
-                grouped = ring.tile([P, QUART, 4], BF16, name=tag, bufs=2, align_bytes=64)
-                nc.vector.tensor_copy(
-                    grouped[:].rearrange("p (c i) t -> p c t i", i=4),
-                    source[:, :, k * QUART : (k + 1) * QUART].rearrange("p t (c i) -> p c t i", i=4),
-                )
-                quantise(up_words[g][k][:], up_plane[g][k][:], grouped[:].rearrange("p c t -> p (c t)"))
+        def quantise_up(c):
+            if c <= NT // 2:
+                grouped = ring.tile([P, RP * P, 4], BF16, name="stage%d" % (c >= 3), bufs=2, align_bytes=64)
+            else:
+                grouped = held([P, RP * P, 4], BF16, "up_words%d" % (c - 3))
+            n0 = c * P % HALF
+            copy = nc.vector.tensor_copy if c < 3 else nc.scalar.copy
+            copy(
+                grouped[:].rearrange("p (g c i) t -> p g c t i", g=RP, i=4),
+                up_raw[c * P // HALF][:, :, :, n0 : n0 + P].rearrange("p g t (c i) -> p g c t i", i=4),
+            )
+            quantise(
+                up_words[c][:].rearrange("p g m -> p (g m)"),
+                up_plane[c][:].rearrange("p g m -> p (g m)"),
+                grouped[:].rearrange("p c t -> p (c t)"),
+            )
 
         def relu(acc, on_vector=False):
             flat = ring.tile([P, HALF], BF16, name="flat", bufs=12, align_bytes=64)
@@ -220,7 +234,11 @@ def tile_list_xcross_relu_kernel(
         for c in range(LATE_X0, NT):
             load_x0(c)
         flats = [[[relu(acc, g == 1) for acc in first[g]] for g in range(RP)], []]
-        quantise_up(0, "stage1")
+        picked = {}
+        for c in range(2):
+            whole = held([P, J], F32, "picked%d" % c)
+            nc.vector.tensor_copy(whole[:], listed(x0[c][:], 0, J))
+            picked[c] = whole
         for g in range(RP):
             made = []
             for u in range(4):
@@ -232,50 +250,74 @@ def tile_list_xcross_relu_kernel(
                 for gg in range(RP):
                     turn(0, gg, flats[0][gg])
             flats[1].append([relu(acc) for acc in made])
-        quantise_up(1, "stage0")
+        for c in (2, 0, 1):
+            quantise_up(c)
         pairs = [held([P, 2, J], F32, "pair%d" % k) for k in range(NT // 2)]
         result = [pairs[c // 2][:, c % 2] for c in range(NT)]
-        order = [(0, 0), (1, 0), (0, 1), (1, 1)] + [(c, s) for c in range(2, NT) for s in range(2)]
-        for step, (c, s) in enumerate(order):
-            if step == 0:
-                for g in range(RP):
-                    turn(1, g, flats[1][g])
+        order = [(2, 0), (0, 0), (1, 0), (2, 1)]
+        order = order + [(c, s) for c in range(3, NT) for s in range(2)] + [(0, 1), (1, 1)]
+        b_t = bank()
+        nc.tensor.transpose(b_t[:, 0:P], b_rows[:], ident[:])
+        bias1 = held([P, NT], F32, "bias1")
+        nc.scalar.activation(bias1[:], b_t[:, 0:NT], ACT.Identity, bias=1.0)
+
+        for g in range(RP):
+            turn(1, g, flats[1][g])
+
+        def y_passes(acc, c, s, which):
             cols = slice(c * P, (c + 1) * P)
-            part_cols = slice(c % 2 * P, (c % 2 + 1) * P)
+            half_cols = slice(c * P % HALF, c * P % HALF + P)
+            for k in which:
+                if k < KP:
+                    operands = (wb[c * P // HALF][:, k, half_cols], wb_plane[4 * k + 4 : P, :].bitcast(U8)[:, cols])
+                    operands = operands + (v_words[s][k][:], v_plane(k, s))
+                else:
+                    g = k - KP
+                    operands = (up_words[c][:, g, :], up_plane[c][:, g, :])
+                    operands = operands + (h_words[s][g][:], h_plane[s][g][:])
+                nc.tensor.matmul_mx(
+                    acc[:],
+                    lhsT=operands[0].bitcast(FP8X4),
+                    lhsT_scale=operands[1],
+                    rhs=operands[2].bitcast(FP8X4),
+                    rhs_scale=operands[3],
+                    start=(k == which[0]),
+                    stop=(k == which[-1]),
+                )
+
+        def cross(acc, c, s, j, width):
+            piece = slice(s * HALF + j, s * HALF + j + width)
+            if c in picked:
+                nc.vector.scalar_tensor_tensor(
+                    result[c][:, piece], acc[:, j : j + width], bias1[:, c : c + 1], picked[c][:, piece], ADD, MULT
+                )
+                return
+            factor = ring.tile([P, HALF], F32, name="factor", bufs=4, align_bytes=64)
+            nc.scalar.activation(factor[:, 0:width], acc[:, j : j + width], ACT.Identity, bias=bias1[:, c : c + 1])
+            nc.vector.tensor_tensor(
+                result[c][:, piece], listed(x0[c][:], s * HALF + j, width), factor[:, 0:width], MULT
+            )
+
+        def store(c, tiles, js):
+            rows_out = out[c * P : (c + tiles) * P, js].rearrange("(k p) j -> p k j", k=tiles)
+            nc.sync.dma_start(rows_out, pairs[c // 2][:, c % 2 : c % 2 + tiles, js])
+
+        for c, s in order:
             acc = bank()
-            for a in range(KP):
-                nc.tensor.matmul_mx(
-                    acc[:],
-                    lhsT=wb[:, a, cols].bitcast(FP8X4),
-                    lhsT_scale=wb_plane[4 * a + 4 : P, :].bitcast(U8)[:, cols],
-                    rhs=v_words[s][a][:].bitcast(FP8X4),
-                    rhs_scale=v_plane(a, s),
-                    start=(a == 0),
-                    stop=False,
-                )
-            for g in range(RP):
-                nc.tensor.matmul_mx(
-                    acc[:],
-                    lhsT=up_words[g][c // 2][:, part_cols].bitcast(FP8X4),
-                    lhsT_scale=up_plane[g][c // 2][:, part_cols],
-                    rhs=h_words[s][g][:].bitcast(FP8X4),
-                    rhs_scale=h_plane[s][g][:],
-                    start=False,
-                    stop=(g == RP - 1),
-                )
-            factor = ring.tile([P, HALF], F32, name="factor", bufs=5, align_bytes=64)
-            width = QUART if step == len(order) - 1 else HALF
+            y_passes(acc, c, s, [0, 1, 2, 3, 4] if c < NT // 2 else [3, 4, 0, 1, 2])
+            width = QUART if (c, s) == order[-1] else HALF
             for j in range(0, HALF, width):
-                piece = slice(s * HALF + j, s * HALF + j + width)
-                part = slice(j, j + width)
-                nc.scalar.activation(factor[:, part], acc[:, part], ACT.Identity, bias=bias1[:, c : c + 1])
-                nc.vector.tensor_tensor(
-                    result[c][:, piece], listed(x0[c][:], s * HALF + j, width), factor[:, part], MULT
-                )
-                if c == NT - 1:
-                    nc.sync.dma_start(out[cols, piece], result[c][:, piece])
-            if c == NT - 2 and s == 1:
-                nc.sync.dma_start(out[cols, :], result[c])
-            if c in (1, 3, 5) and s == 1:
-                rows_out = out[(c - 1) * P : (c + 1) * P, :].rearrange("(k p) j -> p k j", k=2)
-                nc.sync.dma_start(rows_out, pairs[c // 2][:])
+                cross(acc, c, s, j, width)
+                if c < 2 and s == 1:
+                    store(c, 1, slice(HALF + j, HALF + j + width))
+            if (c, s) == (2, 0):
+                for cc in (3, 4):
+                    quantise_up(cc)
+            if 2 <= c <= 4 and s == 1:
+                quantise_up(c + 3)
+            if (c, s) == (1, 0):
+                store(0, 2, slice(0, HALF))
+            if c in (3, 5) and s == 1:
+                store(c - 1, 2, slice(0, J))
+            if c >= 6 and s == 1:
+                store(c, 1, slice(0, J))

@@ -26,7 +26,7 @@ NT = N // P
 HALF = 512
 QUART = 256
 LATE_X0 = 5
-LATE_WORDS = T + R // 2 + KP * N + RP * 4 * N + LATE_X0 * T
+LATE_WORDS = T + KP * N + RP * 4 * N + LATE_X0 * T
 
 
 def tile_list_xcross_relu_kernel(
@@ -50,42 +50,41 @@ def tile_list_xcross_relu_kernel(
         wb_plane = held([P, N // 4], I32, "wb_plane")
         b_rows = held([P, P], F32, "b_rows")
         ident = held([P, P], F32, "ident")
-        dn = [held([P, R // 2], I32, "dn%d" % a) for a in range(KP - 1)]
+        dn_first = held([P, R // 2], I32, "dn_first")
+        dn_rest = held([P, KP - 1, R // 2], I32, "dn_rest")
+        dn = [dn_first[:]] + [dn_rest[:, a - 1] for a in range(1, KP)]
         tab_win = [held([P, T], I32, "window%d" % a) for a in range(KP - 1)]
         with tc.tile_pool(name="head", bufs=1) as head_pool:
             space = head_pool.tile([P, LATE_WORDS], I32, name="space", align_bytes=64)
             tab_rows = space[:, 0 : T // 4]
 
-            nc.vector.memset(dn_plane[:], 0)
+            nc.gpsimd.memset(dn_plane[:], 0)
             nc.vector.memset(v_moved[:], 0)
-            nc.gpsimd.memset(b_rows[:], 0.0)
-            nc.gpsimd.dma_start(b_rows[0:NT, :], b.rearrange("(c p) -> c p", p=P))
-            nc.gpsimd.memset(wb_plane[:], 0)
+            nc.vector.memset(wb_plane[:], 0)
+            nc.vector.memset(b_rows[:], 0.0)
+            dn_rows = dn_scales.rearrange("a (q r) n -> r q a n", r=4)
             make_identity(nc, ident[:])
             for q in range(4):
                 nc.gpsimd.dma_start(
                     wb_plane[32 * q + 4 : 32 * q + 16, :], wb_scales[:, 4 * q : 4 * q + 4, :].bitcast(I32)
                 )
+            nc.gpsimd.dma_start(b_rows[0:NT, :], b.rearrange("(c p) -> c p", p=P))
             nc.sync.dma_start(offsets[:], offs)
             rows = tab_scales.rearrange("a q t -> (a q) t").bitcast(I32)
-            for q in range(3):
+            for q in (0, 2, 1):
                 nc.sync.dma_start(tab_rows[32 * q : 32 * q + 32, :], rows[4 * q : 4 * q + 32, :])
             nc.sync.dma_start(tab_rows[96:112, :], rows[12:28, :])
             nc.sync.dma_start(tab_rows[112:128, :], rows[32:48, :])
-            dn_rows = dn_scales.rearrange("a (q r) n -> r q a n", r=4)
 
             def load_table(a):
                 nc.sync.dma_start(tab_win[a][:], tab_words[a].rearrange("p t i -> p (t i)").bitcast(I32))
 
-            def load_dn(a):
-                nc.sync.dma_start(dn[a][:], dn_words[a].bitcast(I32))
-
             load_table(0)
-            load_dn(0)
+            nc.sync.dma_start(dn_first[:], dn_words[0].bitcast(I32))
             for r in range(4):
                 nc.sync.dma_start(dn_plane[r:P:32], dn_rows[r].bitcast(I32))
             load_table(1)
-            load_dn(1)
+            nc.sync.dma_start(dn_rest[:], dn_words[1:KP].rearrange("a p w -> p a w").bitcast(I32))
 
             def listed(window, j0, width):
                 return window.indirect(offsets[:, j0 // 16 : (j0 + width) // 16])
@@ -105,10 +104,8 @@ def tile_list_xcross_relu_kernel(
                 )
 
         tab_win.append(late_tile([P, T], I32, "window2"))
-        dn.append(late_tile([P, R // 2], I32, "dn2"))
         move_rows(1)
         load_table(2)
-        load_dn(2)
         move_rows(2)
         v_words = [[held([P, HALF], U32, "v_words%d_%d" % (s, a)) for a in range(KP)] for s in range(2)]
 
@@ -149,8 +146,9 @@ def tile_list_xcross_relu_kernel(
             nc.sync.dma_start(win[:], x0T[c * P : (c + 1) * P, :])
             x0.append(win)
 
-        for c in range(2):
-            load_x0(c)
+        x0_early = late_tile([P, 2, T], F32, "x0_early")
+        nc.sync.dma_start(x0_early[:], x0T[0 : 2 * P, :].rearrange("(k p) t -> p k t", k=2))
+        x0.extend([x0_early[:, 0], x0_early[:, 1]])
         load_up(0)
         load_wb(0)
         load_x0(2)
@@ -237,7 +235,7 @@ def tile_list_xcross_relu_kernel(
         picked = {}
         for c in range(2):
             whole = held([P, J], F32, "picked%d" % c)
-            nc.vector.tensor_copy(whole[:], listed(x0[c][:], 0, J))
+            nc.vector.tensor_copy(whole[:], listed(x0[c], 0, J))
             picked[c] = whole
         for g in range(RP):
             made = []

@@ -16,7 +16,6 @@ FP8X4 = mybir.dt.float8_e4m3fn_x4
 FP4X4 = mybir.dt.float4_e2m1fn_x4
 ACT = mybir.ActivationFunctionType
 MULT = mybir.AluOpType.mult
-ADD = mybir.AluOpType.add
 MAX = mybir.AluOpType.max
 
 P = 128
@@ -25,8 +24,9 @@ RP = R // 512
 NT = N // P
 HALF = 512
 QUART = 256
-LATE_X0 = 5
-LATE_WORDS = T + KP * N + RP * 4 * N + LATE_X0 * T
+OWN_X0 = 5
+LATE_WORDS = T + KP * N + RP * 4 * N + OWN_X0 * T
+STORES = ((0, 4), (4, 2), (6, 1), (7, 1))
 
 
 def tile_list_xcross_relu_kernel(
@@ -52,23 +52,23 @@ def tile_list_xcross_relu_kernel(
         ident = held([P, P], F32, "ident")
         dn_first = held([P, R // 2], I32, "dn_first")
         dn_rest = held([P, KP - 1, R // 2], I32, "dn_rest")
-        dn = [dn_first[:]] + [dn_rest[:, a - 1] for a in range(1, KP)]
+        dn_raw = [dn_first[:]] + [dn_rest[:, a - 1] for a in range(1, KP)]
         tab_win = [held([P, T], I32, "window%d" % a) for a in range(KP - 1)]
         with tc.tile_pool(name="head", bufs=1) as head_pool:
             space = head_pool.tile([P, LATE_WORDS], I32, name="space", align_bytes=64)
             tab_rows = space[:, 0 : T // 4]
 
             nc.gpsimd.memset(dn_plane[:], 0)
-            nc.vector.memset(v_moved[:], 0)
-            nc.vector.memset(wb_plane[:], 0)
             nc.vector.memset(b_rows[:], 0.0)
+            nc.vector.memset(wb_plane[:], 0)
+            nc.vector.memset(v_moved[:], 0)
             dn_rows = dn_scales.rearrange("a (q r) n -> r q a n", r=4)
             make_identity(nc, ident[:])
+            nc.gpsimd.dma_start(b_rows[0:NT, :], b.rearrange("(c p) -> c p", p=P))
             for q in range(4):
                 nc.gpsimd.dma_start(
                     wb_plane[32 * q + 4 : 32 * q + 16, :], wb_scales[:, 4 * q : 4 * q + 4, :].bitcast(I32)
                 )
-            nc.gpsimd.dma_start(b_rows[0:NT, :], b.rearrange("(c p) -> c p", p=P))
             nc.sync.dma_start(offsets[:], offs)
             rows = tab_scales.rearrange("a q t -> (a q) t").bitcast(I32)
             for q in (0, 2, 1):
@@ -107,6 +107,35 @@ def tile_list_xcross_relu_kernel(
         move_rows(1)
         load_table(2)
         move_rows(2)
+
+        wb = late_tile([P, KP, N], I32, "wb")
+        nc.sync.dma_start(wb[:], wb_words.rearrange("a p n i -> p a (n i)").bitcast(I32))
+        up_rows = upw.rearrange("(g p t) n -> g p (t n)", g=RP, t=4)
+        up_raw = []
+        for g in range(RP):
+            raw = late_tile([P, 4 * N], F32, "up_raw%d" % g)
+            nc.sync.dma_start(raw[:], up_rows[g])
+            up_raw.append(raw[:].rearrange("p (t n) -> p t n", t=4))
+        x0 = []
+
+        def load_x0(c):
+            if c < OWN_X0:
+                win = late_tile([P, T], F32, "x0_%d" % c)
+            elif c < NT - 1:
+                win = held([P, T], F32, "window%d" % (c - OWN_X0))
+            else:
+                win = late_tile([P, T], F32, "window2")
+            nc.sync.dma_start(win[:], x0T[c * P : (c + 1) * P, :])
+            x0.append(win)
+
+        for c in range(OWN_X0):
+            load_x0(c)
+
+        b_t = bank()
+        nc.tensor.transpose(b_t[:, 0:P], b_rows[:], ident[:])
+        bias1 = held([P, NT], F32, "bias1")
+        nc.scalar.activation(bias1[:], b_t[:, 0:NT], ACT.Identity, bias=1.0)
+
         v_words = [[held([P, HALF], U32, "v_words%d_%d" % (s, a)) for a in range(KP)] for s in range(2)]
 
         def gather(a, s, width=HALF):
@@ -119,159 +148,116 @@ def tile_list_xcross_relu_kernel(
             plane = v_rows[:] if a == 0 else v_moved[:, a - 1, :].bitcast(U8)
             return plane[:, s * HALF : (s + 1) * HALF]
 
-        wb = []
-        up_rows = upw.rearrange("(g p t) n -> g p t n", g=RP, t=4)
-        wb_rows = wb_words.rearrange("a p n i -> p a (n i)").bitcast(I32)
-        up_raw = []
-        x0 = []
+        dn = [[held([P, HALF], U16, "dn%d_%d" % (a, g)) for g in range(RP)] for a in range(KP)]
+        dn_scale = [held([P, R], U8, "dn_scale%d" % a) for a in range(KP)]
 
-        def load_up(s):
-            raw = late_tile([P, RP, 4, HALF], F32, "up_raw%d" % s)
+        def deal_dn(a):
             for g in range(RP):
-                nc.sync.dma_start(raw[:, g], up_rows[g][:, :, s * HALF : (s + 1) * HALF])
-            up_raw.append(raw)
-
-        def load_wb(s):
-            words = late_tile([P, KP, HALF], I32, "wb%d" % s)
-            nc.sync.dma_start(words[:], wb_rows[:, :, s * HALF : (s + 1) * HALF])
-            wb.append(words)
-
-        def load_x0(c):
-            if c < LATE_X0:
-                win = late_tile([P, T], F32, "x0_%d" % c)
-            elif c < NT - 1:
-                win = held([P, T], F32, "window%d" % (c - LATE_X0))
-            else:
-                win = late_tile([P, T], F32, "window2")
-            nc.sync.dma_start(win[:], x0T[c * P : (c + 1) * P, :])
-            x0.append(win)
-
-        x0_early = late_tile([P, 2, T], F32, "x0_early")
-        nc.sync.dma_start(x0_early[:], x0T[0 : 2 * P, :].rearrange("(k p) t -> p k t", k=2))
-        x0.extend([x0_early[:, 0], x0_early[:, 1]])
-        load_up(0)
-        load_wb(0)
-        load_x0(2)
-        load_up(1)
-        load_x0(3)
-        load_wb(1)
-        for c in range(4, LATE_X0):
-            load_x0(c)
-
-        def dn_pass(acc, a, g, s, u):
-            js = slice(u * P, (u + 1) * P)
-            nc.tensor.matmul_mx(
-                acc[:],
-                lhsT=v_words[s][a][:, js].bitcast(FP8X4),
-                lhsT_scale=v_plane(a, s)[:, js],
-                rhs=dn[a][:, g * QUART : (g + 1) * QUART].bitcast(FP4X4),
-                rhs_scale=dn_plane[:, a, g * P : (g + 1) * P].bitcast(U8),
-                start=(a == 0),
-                stop=(a == KP - 1),
+                nc.scalar.copy(
+                    dn[a][g][:].rearrange("p (t b m) -> p b t m", t=4, m=8),
+                    dn_raw[a].bitcast(U16)[:, g * HALF : (g + 1) * HALF].rearrange("p (b m t) -> p b t m", m=8, t=4),
+                )
+            nc.vector.tensor_copy(
+                dn_scale[a][:].rearrange("p (g t b m) -> p g b t m", g=RP, t=4, m=16),
+                dn_plane[:, a, :].bitcast(U8).rearrange("p (g b m t) -> p g b t m", g=RP, m=16, t=4),
             )
+
+        def dn_passes(acc, a, s, q, g, pair):
+            js = slice(q * QUART, (q + 1) * QUART)
+            for e in range(2):
+                t = 2 * pair + e
+                nc.tensor.matmul_mx(
+                    acc[:, e * QUART : (e + 1) * QUART],
+                    lhsT=dn[a][g][:, t * P : (t + 1) * P].bitcast(FP4X4),
+                    lhsT_scale=dn_scale[a][:, g * HALF + t * P : g * HALF + (t + 1) * P],
+                    rhs=v_words[s][a][:, js].bitcast(FP8X4),
+                    rhs_scale=v_plane(a, s)[:, js],
+                    start=(a == 0 and e == 0),
+                    stop=(a == KP - 1 and e == 1),
+                )
 
         h_words = [[held([P, HALF], U32, "h_words%d_%d" % (s, g)) for g in range(RP)] for s in range(2)]
         h_plane = [[held([P, HALF], U8, "h_plane%d_%d" % (s, g)) for g in range(RP)] for s in range(2)]
-        up_words = [held([P, RP, P], U32, "up_words%d" % c) for c in range(NT)]
-        up_plane = [held([P, RP, P], U8, "up_plane%d" % c) for c in range(NT)]
+        up_words = [held([P, N], U32, "up_words%d" % g) for g in range(RP)]
+        up_plane = [held([P, N], U8, "up_plane%d" % g) for g in range(RP)]
 
         def quantise(words, plane, grouped):
             nc.vector.quantize_mx(out=words.bitcast(FP8X4), scales=plane, in_=grouped)
 
-        def quantise_up(c):
-            if c <= NT // 2:
-                grouped = ring.tile([P, RP * P, 4], BF16, name="stage%d" % (c >= 3), bufs=2, align_bytes=64)
-            else:
-                grouped = held([P, RP * P, 4], BF16, "up_words%d" % (c - 3))
-            n0 = c * P % HALF
-            copy = nc.vector.tensor_copy if c < 3 else nc.scalar.copy
+        def quantise_up(g, n0, width, copy):
+            grouped = ring.tile([P, width, 4], BF16, name="stage%d" % g, bufs=2 + 2 * g, align_bytes=64)
             copy(
-                grouped[:].rearrange("p (g c i) t -> p g c t i", g=RP, i=4),
-                up_raw[c * P // HALF][:, :, :, n0 : n0 + P].rearrange("p g t (c i) -> p g c t i", i=4),
+                grouped[:].rearrange("p (c i) t -> p c t i", i=4),
+                up_raw[g][:, :, n0 : n0 + width].rearrange("p t (c i) -> p c t i", i=4),
             )
             quantise(
-                up_words[c][:].rearrange("p g m -> p (g m)"),
-                up_plane[c][:].rearrange("p g m -> p (g m)"),
+                up_words[g][:, n0 : n0 + width],
+                up_plane[g][:, n0 : n0 + width],
                 grouped[:].rearrange("p c t -> p (c t)"),
             )
 
-        def relu(acc, on_vector=False):
-            flat = ring.tile([P, HALF], BF16, name="flat", bufs=12, align_bytes=64)
-            dst = flat[:].rearrange("j (w p e) -> j w p e", w=2, e=2)
-            src = acc[:].rearrange("j (p w e) -> j w p e", w=2, e=2)
+        def relu(grouped, acc, q, pair, on_vector):
+            dst = grouped[:, q * QUART : (q + 1) * QUART, 2 * pair : 2 * pair + 2]
+            src = acc[:].rearrange("p (e j) -> p j e", e=2)
             if on_vector:
                 nc.vector.tensor_scalar(dst, src, 0.0, None, MAX)
             else:
                 nc.scalar.activation(dst, src, ACT.Relu)
-            return flat
 
-        def turn(s, g, flats):
-            grouped = ring.tile([P, HALF, 2], F32, name="stage%d" % s, bufs=2, align_bytes=64)
-            for pair in range(2):
-                turned = bank()
-                for k in range(2):
-                    for w in range(2):
-                        at = (2 * k + w) * P
-                        words = flats[2 * pair + k][:].bitcast(F32)
-                        nc.tensor.transpose(turned[:, at : at + P], words[:, w * P : (w + 1) * P], ident[:])
-                nc.scalar.copy(
-                    grouped[:, pair * QUART : (pair + 1) * QUART, :].rearrange("p (k j) w -> p k j w", k=2),
-                    turned[:].rearrange("p (k w j) -> p k j w", k=2, w=2),
-                )
-            quantise(h_words[s][g][:], h_plane[s][g][:], grouped[:].rearrange("p j w -> p (j w)").bitcast(BF16))
+        def h_tile():
+            return ring.tile([P, HALF, 4], BF16, name="h", bufs=3, align_bytes=64)
 
-        first = [[bank() for u in range(4)] for g in range(RP)]
+        def quantise_h(s, g, grouped):
+            quantise(h_words[s][g][:], h_plane[s][g][:], grouped[:].rearrange("p j t -> p (j t)"))
+
+        slots = [(q, g, pair) for q in range(2) for g in range(RP) for pair in range(2)]
+        first = {slot: bank() for slot in slots}
         for a in range(KP):
+            deal_dn(a)
             gather(a, 0, HALF if a == 1 else QUART)
-            for pair in range(2):
-                for g in range(RP):
-                    for u in range(2 * pair, 2 * pair + 2):
-                        dn_pass(first[g][u], a, g, 0, u)
+            for q, g, pair in slots:
+                dn_passes(first[q, g, pair], a, 0, q, g, pair)
         for a in range(KP):
             gather(a, 1)
-        for c in range(LATE_X0, NT):
+        for c in range(OWN_X0, NT):
             load_x0(c)
-        flats = [[[relu(acc, g == 1) for acc in first[g]] for g in range(RP)], []]
-        picked = {}
-        for c in range(2):
-            whole = held([P, J], F32, "picked%d" % c)
-            nc.vector.tensor_copy(whole[:], listed(x0[c], 0, J))
-            picked[c] = whole
+        grouped = [h_tile() for g in range(RP)]
+        for q, g, pair in slots:
+            relu(grouped[g], first[q, g, pair], q, pair, g == 1)
         for g in range(RP):
-            made = []
-            for u in range(4):
-                acc = bank()
-                for a in range(KP):
-                    dn_pass(acc, a, g, 1, u)
-                made.append(acc)
-            if g == 0:
-                for gg in range(RP):
-                    turn(0, gg, flats[0][gg])
-            flats[1].append([relu(acc) for acc in made])
-        for c in (2, 0, 1):
-            quantise_up(c)
-        pairs = [held([P, 2, J], F32, "pair%d" % k) for k in range(NT // 2)]
-        result = [pairs[c // 2][:, c % 2] for c in range(NT)]
-        order = [(2, 0), (0, 0), (1, 0), (2, 1)]
-        order = order + [(c, s) for c in range(3, NT) for s in range(2)] + [(0, 1), (1, 1)]
-        b_t = bank()
-        nc.tensor.transpose(b_t[:, 0:P], b_rows[:], ident[:])
-        bias1 = held([P, NT], F32, "bias1")
-        nc.scalar.activation(bias1[:], b_t[:, 0:NT], ACT.Identity, bias=1.0)
-
+            quantise_h(0, g, grouped[g])
         for g in range(RP):
-            turn(1, g, flats[1][g])
+            tile = h_tile()
+            for q in range(2):
+                for pair in range(2):
+                    acc = bank()
+                    for a in range(KP):
+                        dn_passes(acc, a, 1, q, g, pair)
+                    relu(tile, acc, q, pair, False)
+            quantise_h(1, g, tile)
+        for n0 in range(0, N, HALF):
+            quantise_up(0, n0, HALF, nc.vector.tensor_copy)
+        quantise_up(1, 0, P, nc.vector.tensor_copy)
 
-        def y_passes(acc, c, s, which):
+        result = []
+        stored = {}
+        for c0, tiles in STORES:
+            if c0 == 0:
+                whole = late_tile([P, tiles, J], F32, "up_raw0")
+            else:
+                whole = held([P, tiles, J], F32, "result%d" % c0)
+            result.extend(whole[:, k] for k in range(tiles))
+            stored[c0 + tiles - 1] = (c0, tiles, whole)
+
+        def y_passes(acc, c, s):
             cols = slice(c * P, (c + 1) * P)
-            half_cols = slice(c * P % HALF, c * P % HALF + P)
-            for k in which:
+            for k in range(KP + RP):
                 if k < KP:
-                    operands = (wb[c * P // HALF][:, k, half_cols], wb_plane[4 * k + 4 : P, :].bitcast(U8)[:, cols])
+                    operands = (wb[:, k, cols], wb_plane[4 * k + 4 : P, :].bitcast(U8)[:, cols])
                     operands = operands + (v_words[s][k][:], v_plane(k, s))
                 else:
                     g = k - KP
-                    operands = (up_words[c][:, g, :], up_plane[c][:, g, :])
+                    operands = (up_words[g][:, cols], up_plane[g][:, cols])
                     operands = operands + (h_words[s][g][:], h_plane[s][g][:])
                 nc.tensor.matmul_mx(
                     acc[:],
@@ -279,43 +265,22 @@ def tile_list_xcross_relu_kernel(
                     lhsT_scale=operands[1],
                     rhs=operands[2].bitcast(FP8X4),
                     rhs_scale=operands[3],
-                    start=(k == which[0]),
-                    stop=(k == which[-1]),
+                    start=(k == 0),
+                    stop=(k == KP + RP - 1),
                 )
 
-        def cross(acc, c, s, j, width):
-            piece = slice(s * HALF + j, s * HALF + j + width)
-            if c in picked:
-                nc.vector.scalar_tensor_tensor(
-                    result[c][:, piece], acc[:, j : j + width], bias1[:, c : c + 1], picked[c][:, piece], ADD, MULT
+        for c in range(NT):
+            if c + 1 < NT:
+                quantise_up(1, (c + 1) * P, P, nc.scalar.copy)
+            for s in range(2):
+                acc = bank()
+                y_passes(acc, c, s)
+                factor = ring.tile([P, HALF], F32, name="factor", bufs=6, align_bytes=64)
+                nc.scalar.activation(factor[:], acc[:], ACT.Identity, bias=bias1[:, c : c + 1])
+                nc.vector.tensor_tensor(
+                    result[c][:, s * HALF : (s + 1) * HALF], listed(x0[c][:], s * HALF, HALF), factor[:], MULT
                 )
-                return
-            factor = ring.tile([P, HALF], F32, name="factor", bufs=4, align_bytes=64)
-            nc.scalar.activation(factor[:, 0:width], acc[:, j : j + width], ACT.Identity, bias=bias1[:, c : c + 1])
-            nc.vector.tensor_tensor(
-                result[c][:, piece], listed(x0[c][:], s * HALF + j, width), factor[:, 0:width], MULT
-            )
-
-        def store(c, tiles, js):
-            rows_out = out[c * P : (c + tiles) * P, js].rearrange("(k p) j -> p k j", k=tiles)
-            nc.sync.dma_start(rows_out, pairs[c // 2][:, c % 2 : c % 2 + tiles, js])
-
-        for c, s in order:
-            acc = bank()
-            y_passes(acc, c, s, [0, 1, 2, 3, 4] if c < NT // 2 else [3, 4, 0, 1, 2])
-            width = QUART if (c, s) == order[-1] else HALF
-            for j in range(0, HALF, width):
-                cross(acc, c, s, j, width)
-                if c < 2 and s == 1:
-                    store(c, 1, slice(HALF + j, HALF + j + width))
-            if (c, s) == (2, 0):
-                for cc in (3, 4):
-                    quantise_up(cc)
-            if 2 <= c <= 4 and s == 1:
-                quantise_up(c + 3)
-            if (c, s) == (1, 0):
-                store(0, 2, slice(0, HALF))
-            if c in (3, 5) and s == 1:
-                store(c - 1, 2, slice(0, J))
-            if c >= 6 and s == 1:
-                store(c, 1, slice(0, J))
+            if c in stored:
+                c0, tiles, whole = stored[c]
+                rows_out = out[c0 * P : (c0 + tiles) * P, :].rearrange("(k p) j -> p k j", k=tiles)
+                nc.sync.dma_start(rows_out, whole[:])

@@ -16,7 +16,7 @@ FP8X4 = mybir.dt.float8_e4m3fn_x4
 FP4X4 = mybir.dt.float4_e2m1fn_x4
 ACT = mybir.ActivationFunctionType
 MULT = mybir.AluOpType.mult
-MAX = mybir.AluOpType.max
+ADD = mybir.AluOpType.add
 
 P = 128
 KP = K // 512
@@ -26,7 +26,8 @@ HALF = 512
 QUART = 256
 OWN_X0 = 5
 LATE_WORDS = T + KP * N + RP * 4 * N + OWN_X0 * T
-STORES = ((0, 4), (4, 2), (6, 1), (7, 1))
+STORES = ((0, 1), (1, 3), (4, 2), (6, 1), (7, 1))
+Y_BANKS = 4
 
 
 def tile_list_xcross_relu_kernel(
@@ -36,13 +37,13 @@ def tile_list_xcross_relu_kernel(
     with ExitStack() as ctx:
         keep = ctx.enter_context(tc.tile_pool(name="keep", bufs=1))
         ring = ctx.enter_context(tc.tile_pool(name="ring", bufs=2))
-        psum = ctx.enter_context(tc.psum_pool(name="psum", bufs=8))
+        psum = ctx.enter_context(tc.psum_pool(name="psum", bufs=1))
 
         def held(shape, dtype, name):
             return keep.tile(shape, dtype, name=name, align_bytes=64)
 
-        def bank():
-            return psum.tile([P, HALF], F32, name="bank")
+        def bank(n):
+            return psum.tile([P, HALF], F32, name="bank%d" % n)
 
         offsets = keep.tile([P, J // 16], U16, name="offsets")
         v_moved = held([P, KP - 1, J // 4], I32, "v_moved")
@@ -108,15 +109,23 @@ def tile_list_xcross_relu_kernel(
         load_table(2)
         move_rows(2)
 
-        wb = late_tile([P, KP, N], I32, "wb")
-        nc.sync.dma_start(wb[:], wb_words.rearrange("a p n i -> p a (n i)").bitcast(I32))
-        up_rows = upw.rearrange("(g p t) n -> g p (t n)", g=RP, t=4)
-        up_raw = []
-        for g in range(RP):
-            raw = late_tile([P, 4 * N], F32, "up_raw%d" % g)
-            nc.sync.dma_start(raw[:], up_rows[g])
-            up_raw.append(raw[:].rearrange("p (t n) -> p t n", t=4))
+        wb_rows = wb_words.rearrange("a p n i -> p a (n i)").bitcast(I32)
+        up_rows = upw.rearrange("(g p t) n -> g p t n", g=RP, t=4)
+        up_raw = [[], []]
+        wb = []
         x0 = []
+
+        def load_up(side):
+            for g in range(RP):
+                raw = late_tile([P, 4, HALF], F32, "up_raw%d_%d" % (g, side))
+                nc.sync.dma_start(raw[:], up_rows[g][:, :, side * HALF : (side + 1) * HALF])
+                up_raw[g].append(raw[:])
+
+        def load_wb(side):
+            cols = slice(side * HALF, (side + 1) * HALF)
+            words = late_tile([P, KP, HALF], I32, "wb%d" % side)
+            nc.sync.dma_start(words[:], wb_rows[:, :, cols])
+            wb.append(words)
 
         def load_x0(c):
             if c < OWN_X0:
@@ -128,15 +137,16 @@ def tile_list_xcross_relu_kernel(
             nc.sync.dma_start(win[:], x0T[c * P : (c + 1) * P, :])
             x0.append(win)
 
-        for c in range(OWN_X0):
+        load_up(0)
+        load_wb(0)
+        for c in range(NT // 2):
             load_x0(c)
+        load_up(1)
+        load_wb(1)
+        load_x0(4)
 
-        b_t = bank()
-        nc.tensor.transpose(b_t[:, 0:P], b_rows[:], ident[:])
-        bias1 = held([P, NT], F32, "bias1")
-        nc.scalar.activation(bias1[:], b_t[:, 0:NT], ACT.Identity, bias=1.0)
-
-        v_words = [[held([P, HALF], U32, "v_words%d_%d" % (s, a)) for a in range(KP)] for s in range(2)]
+        v_words = [[held([P, HALF], U32, "v_words0_%d" % a) for a in range(KP)], [None]]
+        v_words[1].extend(held([P, HALF], U32, "v_words1_%d" % a) for a in range(1, KP))
 
         def gather(a, s, width=HALF):
             for j in range(0, HALF, width):
@@ -149,7 +159,7 @@ def tile_list_xcross_relu_kernel(
             return plane[:, s * HALF : (s + 1) * HALF]
 
         dn = [[held([P, HALF], U16, "dn%d_%d" % (a, g)) for g in range(RP)] for a in range(KP)]
-        dn_scale = [held([P, R], U8, "dn_scale%d" % a) for a in range(KP)]
+        dn_scale = [[held([P, HALF], U8, "dn_scale%d_%d" % (a, g)) for g in range(RP)] for a in range(KP)]
 
         def deal_dn(a):
             for g in range(RP):
@@ -157,10 +167,10 @@ def tile_list_xcross_relu_kernel(
                     dn[a][g][:].rearrange("p (t b m) -> p b t m", t=4, m=8),
                     dn_raw[a].bitcast(U16)[:, g * HALF : (g + 1) * HALF].rearrange("p (b m t) -> p b t m", m=8, t=4),
                 )
-            nc.vector.tensor_copy(
-                dn_scale[a][:].rearrange("p (g t b m) -> p g b t m", g=RP, t=4, m=16),
-                dn_plane[:, a, :].bitcast(U8).rearrange("p (g b m t) -> p g b t m", g=RP, m=16, t=4),
-            )
+                nc.vector.tensor_copy(
+                    dn_scale[a][g][:].rearrange("p (t b m) -> p b t m", t=4, m=16),
+                    dn_plane[:, a, g * P : (g + 1) * P].bitcast(U8).rearrange("p (b m t) -> p b t m", m=16, t=4),
+                )
 
         def dn_passes(acc, a, s, q, g, pair):
             js = slice(q * QUART, (q + 1) * QUART)
@@ -169,7 +179,7 @@ def tile_list_xcross_relu_kernel(
                 nc.tensor.matmul_mx(
                     acc[:, e * QUART : (e + 1) * QUART],
                     lhsT=dn[a][g][:, t * P : (t + 1) * P].bitcast(FP4X4),
-                    lhsT_scale=dn_scale[a][:, g * HALF + t * P : g * HALF + (t + 1) * P],
+                    lhsT_scale=dn_scale[a][g][:, t * P : (t + 1) * P],
                     rhs=v_words[s][a][:, js].bitcast(FP8X4),
                     rhs_scale=v_plane(a, s)[:, js],
                     start=(a == 0 and e == 0),
@@ -178,87 +188,105 @@ def tile_list_xcross_relu_kernel(
 
         h_words = [[held([P, HALF], U32, "h_words%d_%d" % (s, g)) for g in range(RP)] for s in range(2)]
         h_plane = [[held([P, HALF], U8, "h_plane%d_%d" % (s, g)) for g in range(RP)] for s in range(2)]
-        up_words = [held([P, N], U32, "up_words%d" % g) for g in range(RP)]
-        up_plane = [held([P, N], U8, "up_plane%d" % g) for g in range(RP)]
+        up_codes = {}
 
         def quantise(words, plane, grouped):
             nc.vector.quantize_mx(out=words.bitcast(FP8X4), scales=plane, in_=grouped)
 
         def quantise_up(g, n0, width, copy):
-            grouped = ring.tile([P, width, 4], BF16, name="stage%d" % g, bufs=2 + 2 * g, align_bytes=64)
+            grouped = ring.tile([P, width, 4], BF16, name="stage", bufs=2, align_bytes=64)
             copy(
                 grouped[:].rearrange("p (c i) t -> p c t i", i=4),
-                up_raw[g][:, :, n0 : n0 + width].rearrange("p t (c i) -> p c t i", i=4),
+                up_raw[g][n0 // HALF][:, :, n0 % HALF : n0 % HALF + width].rearrange("p t (c i) -> p c t i", i=4),
             )
-            quantise(
-                up_words[g][:, n0 : n0 + width],
-                up_plane[g][:, n0 : n0 + width],
-                grouped[:].rearrange("p c t -> p (c t)"),
-            )
+            words = held([P, width], U32, "up_words%d_%d" % (g, n0))
+            plane = held([P, width], U8, "up_plane%d_%d" % (g, n0))
+            quantise(words[:], plane[:], grouped[:].rearrange("p c t -> p (c t)"))
+            for at in range(0, width, P):
+                up_codes[g, (n0 + at) // P] = (words[:, at : at + P], plane[:, at : at + P])
 
-        def relu(grouped, acc, q, pair, on_vector):
+        def relu(grouped, acc, q, pair):
             dst = grouped[:, q * QUART : (q + 1) * QUART, 2 * pair : 2 * pair + 2]
-            src = acc[:].rearrange("p (e j) -> p j e", e=2)
-            if on_vector:
-                nc.vector.tensor_scalar(dst, src, 0.0, None, MAX)
-            else:
-                nc.scalar.activation(dst, src, ACT.Relu)
+            nc.scalar.activation(dst, acc[:].rearrange("p (e j) -> p j e", e=2), ACT.Relu)
 
-        def h_tile():
-            return ring.tile([P, HALF, 4], BF16, name="h", bufs=3, align_bytes=64)
+        def h_tile(s, g):
+            return held([P, HALF, 4], BF16, "h%d_%d" % (s, g))
 
         def quantise_h(s, g, grouped):
             quantise(h_words[s][g][:], h_plane[s][g][:], grouped[:].rearrange("p j t -> p (j t)"))
 
-        slots = [(q, g, pair) for q in range(2) for g in range(RP) for pair in range(2)]
-        first = {slot: bank() for slot in slots}
+        slots = [(g, u) for half in range(2) for g in range(RP) for u in (2 * half, 2 * half + 1)]
+        first = {slot: bank(n) for n, slot in enumerate(slots)}
         for a in range(KP):
             deal_dn(a)
             gather(a, 0, HALF if a == 1 else QUART)
-            for q, g, pair in slots:
-                dn_passes(first[q, g, pair], a, 0, q, g, pair)
+            for g, u in slots:
+                js = slice(u * P, (u + 1) * P)
+                for t in range(4):
+                    nc.tensor.matmul_mx(
+                        first[g, u][:, t * P : (t + 1) * P],
+                        lhsT=dn[a][g][:, t * P : (t + 1) * P].bitcast(FP4X4),
+                        lhsT_scale=dn_scale[a][g][:, t * P : (t + 1) * P],
+                        rhs=v_words[0][a][:, js].bitcast(FP8X4),
+                        rhs_scale=v_plane(a, 0)[:, js],
+                        start=(a == 0 and t == 0),
+                        stop=(a == KP - 1 and t == 3),
+                    )
+        v_words[1][0] = held([P, HALF], U32, "dn_plane")
         for a in range(KP):
             gather(a, 1)
         for c in range(OWN_X0, NT):
             load_x0(c)
-        grouped = [h_tile() for g in range(RP)]
-        for q, g, pair in slots:
-            relu(grouped[g], first[q, g, pair], q, pair, g == 1)
+        grouped = [h_tile(0, g) for g in range(RP)]
+        for g, u in slots:
+            nc.scalar.activation(
+                grouped[g][:, u * P : (u + 1) * P, :], first[g, u][:].rearrange("p (t j) -> p j t", t=4), ACT.Relu
+            )
         for g in range(RP):
             quantise_h(0, g, grouped[g])
         for g in range(RP):
-            tile = h_tile()
-            for q in range(2):
-                for pair in range(2):
-                    acc = bank()
-                    for a in range(KP):
-                        dn_passes(acc, a, 1, q, g, pair)
-                    relu(tile, acc, q, pair, False)
-            quantise_h(1, g, tile)
-        for n0 in range(0, N, HALF):
-            quantise_up(0, n0, HALF, nc.vector.tensor_copy)
-        quantise_up(1, 0, P, nc.vector.tensor_copy)
+            quantise_up(g, 0, HALF, nc.vector.tensor_copy)
+        picked = {}
+
+        def pick(c):
+            picked[c] = held([P, HALF], F32, "picked%d" % c)
+            nc.vector.tensor_copy(picked[c][:], listed(x0[c][:], HALF, HALF))
+
+        pairs = [h_tile(1, g) for g in range(RP)]
+
+        def second_half(g, n):
+            q, pair = divmod(n, 2)
+            acc = bank(4 * g + n)
+            for a in range(KP):
+                dn_passes(acc, a, 1, q, g, pair)
+            relu(pairs[g], acc, q, pair)
+            if n == 3:
+                quantise_h(1, g, pairs[g])
+
+        for n in range(4):
+            second_half(0, n)
+        b_t = bank(0)
+        nc.tensor.transpose(b_t[:, 0:P], b_rows[:], ident[:])
+        bias1 = held([P, NT], F32, "bias1")
+        nc.scalar.activation(bias1[:], b_t[:, 0:NT], ACT.Identity, bias=1.0)
 
         result = []
         stored = {}
         for c0, tiles in STORES:
-            if c0 == 0:
-                whole = late_tile([P, tiles, J], F32, "up_raw0")
-            else:
-                whole = held([P, tiles, J], F32, "result%d" % c0)
+            whole = held([P, tiles, J], F32, "result%d" % c0)
             result.extend(whole[:, k] for k in range(tiles))
             stored[c0 + tiles - 1] = (c0, tiles, whole)
 
         def y_passes(acc, c, s):
             cols = slice(c * P, (c + 1) * P)
+            side_cols = slice(c * P % HALF, c * P % HALF + P)
             for k in range(KP + RP):
                 if k < KP:
-                    operands = (wb[:, k, cols], wb_plane[4 * k + 4 : P, :].bitcast(U8)[:, cols])
+                    operands = (wb[c * P // HALF][:, k, side_cols], wb_plane[4 * k + 4 : P, :].bitcast(U8)[:, cols])
                     operands = operands + (v_words[s][k][:], v_plane(k, s))
                 else:
                     g = k - KP
-                    operands = (up_words[g][:, cols], up_plane[g][:, cols])
-                    operands = operands + (h_words[s][g][:], h_plane[s][g][:])
+                    operands = up_codes[g, c] + (h_words[s][g][:], h_plane[s][g][:])
                 nc.tensor.matmul_mx(
                     acc[:],
                     lhsT=operands[0].bitcast(FP8X4),
@@ -269,18 +297,27 @@ def tile_list_xcross_relu_kernel(
                     stop=(k == KP + RP - 1),
                 )
 
-        for c in range(NT):
-            if c + 1 < NT:
-                quantise_up(1, (c + 1) * P, P, nc.scalar.copy)
-            for s in range(2):
-                acc = bank()
-                y_passes(acc, c, s)
-                factor = ring.tile([P, HALF], F32, name="factor", bufs=6, align_bytes=64)
+        order = [(c, 0) for c in range(4)] + [(c, 1) for c in range(1, 4)]
+        order = order + [(c, s) for c in range(4, NT) for s in range(2)] + [(0, 1)]
+        for n, (c, s) in enumerate(order):
+            if n == 0:
+                second_half(1, 0)
+            if n < 3:
+                second_half(1, n + 1)
+            acc = bank((n + 1) % Y_BANKS)
+            y_passes(acc, c, s)
+            js = slice(s * HALF, (s + 1) * HALF)
+            if s == 1 and c in picked:
+                nc.vector.scalar_tensor_tensor(result[c][:, js], acc[:], bias1[:, c : c + 1], picked[c][:], ADD, MULT)
+            else:
+                factor = ring.tile([P, HALF], F32, name="factor", bufs=4, align_bytes=64)
                 nc.scalar.activation(factor[:], acc[:], ACT.Identity, bias=bias1[:, c : c + 1])
-                nc.vector.tensor_tensor(
-                    result[c][:, s * HALF : (s + 1) * HALF], listed(x0[c][:], s * HALF, HALF), factor[:], MULT
-                )
-            if c in stored:
+                nc.vector.tensor_tensor(result[c][:, js], listed(x0[c][:], s * HALF, HALF), factor[:], MULT)
+            if n < 4:
+                pick(c)
+            if 3 <= n < 7:
+                quantise_up((n - 3) % 2, HALF + (n - 3) // 2 * QUART, QUART, nc.scalar.copy)
+            if s == 1 and c in stored:
                 c0, tiles, whole = stored[c]
                 rows_out = out[c0 * P : (c0 + tiles) * P, :].rearrange("(k p) j -> p k j", k=tiles)
                 nc.sync.dma_start(rows_out, whole[:])

@@ -16,7 +16,7 @@ FP8X4 = mybir.dt.float8_e4m3fn_x4
 FP4X4 = mybir.dt.float4_e2m1fn_x4
 ACT = mybir.ActivationFunctionType
 MULT = mybir.AluOpType.mult
-ADD = mybir.AluOpType.add
+MAX = mybir.AluOpType.max
 
 P = 128
 KP = K // 512
@@ -26,7 +26,7 @@ HALF = 512
 QUART = 256
 OWN_X0 = 5
 LATE_WORDS = T + KP * N + RP * 4 * N + OWN_X0 * T
-STORES = ((0, 1), (1, 3), (4, 2), (6, 1), (7, 1))
+STORES = ((0, 5), (5, 2), (7, 1))
 Y_BANKS = 4
 
 
@@ -109,22 +109,19 @@ def tile_list_xcross_relu_kernel(
         load_table(2)
         move_rows(2)
 
+        up_rows = upw.rearrange("(g p t) n -> g p (t n)", g=RP, t=4)
+        up_raw = []
+        for g in range(RP):
+            raw = late_tile([P, 4 * N], F32, "up_raw%d" % g)
+            nc.sync.dma_start(raw[:], up_rows[g])
+            up_raw.append(raw[:].rearrange("p (t n) -> p t n", t=4))
         wb_rows = wb_words.rearrange("a p n i -> p a (n i)").bitcast(I32)
-        up_rows = upw.rearrange("(g p t) n -> g p t n", g=RP, t=4)
-        up_raw = [[], []]
         wb = []
         x0 = []
 
-        def load_up(side):
-            for g in range(RP):
-                raw = late_tile([P, 4, HALF], F32, "up_raw%d_%d" % (g, side))
-                nc.sync.dma_start(raw[:], up_rows[g][:, :, side * HALF : (side + 1) * HALF])
-                up_raw[g].append(raw[:])
-
         def load_wb(side):
-            cols = slice(side * HALF, (side + 1) * HALF)
             words = late_tile([P, KP, HALF], I32, "wb%d" % side)
-            nc.sync.dma_start(words[:], wb_rows[:, :, cols])
+            nc.sync.dma_start(words[:], wb_rows[:, :, side * HALF : (side + 1) * HALF])
             wb.append(words)
 
         def load_x0(c):
@@ -137,13 +134,10 @@ def tile_list_xcross_relu_kernel(
             nc.sync.dma_start(win[:], x0T[c * P : (c + 1) * P, :])
             x0.append(win)
 
-        load_up(0)
-        load_wb(0)
-        for c in range(NT // 2):
+        for c in range(OWN_X0):
+            if c % 4 == 0:
+                load_wb(c // 4)
             load_x0(c)
-        load_up(1)
-        load_wb(1)
-        load_x0(4)
 
         v_words = [[held([P, HALF], U32, "v_words0_%d" % a) for a in range(KP)], [None]]
         v_words[1].extend(held([P, HALF], U32, "v_words1_%d" % a) for a in range(1, KP))
@@ -186,18 +180,22 @@ def tile_list_xcross_relu_kernel(
                     stop=(a == KP - 1 and e == 1),
                 )
 
-        h_words = [[held([P, HALF], U32, "h_words%d_%d" % (s, g)) for g in range(RP)] for s in range(2)]
+        h_words = [[None] * RP for s in range(2)]
         h_plane = [[held([P, HALF], U8, "h_plane%d_%d" % (s, g)) for g in range(RP)] for s in range(2)]
         up_codes = {}
 
         def quantise(words, plane, grouped):
             nc.vector.quantize_mx(out=words.bitcast(FP8X4), scales=plane, in_=grouped)
 
-        def quantise_up(g, n0, width, copy):
-            grouped = ring.tile([P, width, 4], BF16, name="stage", bufs=2, align_bytes=64)
+        def quantise_up(g, n0, width, on_vector):
+            if on_vector:
+                grouped = held([P, width, 4], BF16, "stage")
+            else:
+                grouped = ring.tile([P, width, 4], BF16, name="factor", bufs=4, align_bytes=64)
+            copy = nc.vector.tensor_copy if on_vector else nc.scalar.copy
             copy(
                 grouped[:].rearrange("p (c i) t -> p c t i", i=4),
-                up_raw[g][n0 // HALF][:, :, n0 % HALF : n0 % HALF + width].rearrange("p t (c i) -> p c t i", i=4),
+                up_raw[g][:, :, n0 : n0 + width].rearrange("p t (c i) -> p c t i", i=4),
             )
             words = held([P, width], U32, "up_words%d_%d" % (g, n0))
             plane = held([P, width], U8, "up_plane%d_%d" % (g, n0))
@@ -213,6 +211,8 @@ def tile_list_xcross_relu_kernel(
             return held([P, HALF, 4], BF16, "h%d_%d" % (s, g))
 
         def quantise_h(s, g, grouped):
+            name = "stage" if (s, g) == (1, 1) else "h_words%d_%d" % (s, g)
+            h_words[s][g] = held([P, HALF], U32, name)
             quantise(h_words[s][g][:], h_plane[s][g][:], grouped[:].rearrange("p j t -> p (j t)"))
 
         slots = [(g, u) for half in range(2) for g in range(RP) for u in (2 * half, 2 * half + 1)]
@@ -239,19 +239,17 @@ def tile_list_xcross_relu_kernel(
             load_x0(c)
         grouped = [h_tile(0, g) for g in range(RP)]
         for g, u in slots:
-            nc.scalar.activation(
-                grouped[g][:, u * P : (u + 1) * P, :], first[g, u][:].rearrange("p (t j) -> p j t", t=4), ACT.Relu
-            )
+            dst = grouped[g][:, u * P : (u + 1) * P, :]
+            src = first[g, u][:].rearrange("p (t j) -> p j t", t=4)
+            if g == 1:
+                nc.vector.tensor_scalar(dst, src, 0.0, None, MAX)
+            else:
+                nc.scalar.activation(dst, src, ACT.Relu)
         for g in range(RP):
             quantise_h(0, g, grouped[g])
-        for g in range(RP):
-            quantise_up(g, 0, HALF, nc.vector.tensor_copy)
-        picked = {}
-
-        def pick(c):
-            picked[c] = held([P, HALF], F32, "picked%d" % c)
-            nc.vector.tensor_copy(picked[c][:], listed(x0[c][:], HALF, HALF))
-
+        quantise_up(0, 0, HALF, True)
+        quantise_up(1, 0, QUART, True)
+        quantise_up(1, QUART, QUART, True)
         pairs = [h_tile(1, g) for g in range(RP)]
 
         def second_half(g, n):
@@ -269,6 +267,8 @@ def tile_list_xcross_relu_kernel(
         nc.tensor.transpose(b_t[:, 0:P], b_rows[:], ident[:])
         bias1 = held([P, NT], F32, "bias1")
         nc.scalar.activation(bias1[:], b_t[:, 0:NT], ACT.Identity, bias=1.0)
+        for n in range(4):
+            second_half(1, n)
 
         result = []
         stored = {}
@@ -277,18 +277,17 @@ def tile_list_xcross_relu_kernel(
             result.extend(whole[:, k] for k in range(tiles))
             stored[c0 + tiles - 1] = (c0, tiles, whole)
 
-        def y_passes(acc, c, s):
+        def y_passes(acc, c, s, js):
             cols = slice(c * P, (c + 1) * P)
-            side_cols = slice(c * P % HALF, c * P % HALF + P)
             for k in range(KP + RP):
                 if k < KP:
-                    operands = (wb[c * P // HALF][:, k, side_cols], wb_plane[4 * k + 4 : P, :].bitcast(U8)[:, cols])
-                    operands = operands + (v_words[s][k][:], v_plane(k, s))
+                    operands = (wb[c // 4][:, k, c % 4 * P : (c % 4 + 1) * P], wb_plane[4 * k + 4 : P, :].bitcast(U8)[:, cols])
+                    operands = operands + (v_words[s][k][:, js], v_plane(k, s)[:, js])
                 else:
                     g = k - KP
-                    operands = up_codes[g, c] + (h_words[s][g][:], h_plane[s][g][:])
+                    operands = up_codes[g, c] + (h_words[s][g][:, js], h_plane[s][g][:, js])
                 nc.tensor.matmul_mx(
-                    acc[:],
+                    acc,
                     lhsT=operands[0].bitcast(FP8X4),
                     lhsT_scale=operands[1],
                     rhs=operands[2].bitcast(FP8X4),
@@ -297,27 +296,20 @@ def tile_list_xcross_relu_kernel(
                     stop=(k == KP + RP - 1),
                 )
 
-        order = [(c, 0) for c in range(4)] + [(c, 1) for c in range(1, 4)]
-        order = order + [(c, s) for c in range(4, NT) for s in range(2)] + [(0, 1)]
-        for n, (c, s) in enumerate(order):
-            if n == 0:
-                second_half(1, 0)
-            if n < 3:
-                second_half(1, n + 1)
-            acc = bank((n + 1) % Y_BANKS)
-            y_passes(acc, c, s)
-            js = slice(s * HALF, (s + 1) * HALF)
-            if s == 1 and c in picked:
-                nc.vector.scalar_tensor_tensor(result[c][:, js], acc[:], bias1[:, c : c + 1], picked[c][:], ADD, MULT)
-            else:
-                factor = ring.tile([P, HALF], F32, name="factor", bufs=4, align_bytes=64)
-                nc.scalar.activation(factor[:], acc[:], ACT.Identity, bias=bias1[:, c : c + 1])
-                nc.vector.tensor_tensor(result[c][:, js], listed(x0[c][:], s * HALF, HALF), factor[:], MULT)
-            if n < 4:
-                pick(c)
-            if 3 <= n < 7:
-                quantise_up((n - 3) % 2, HALF + (n - 3) // 2 * QUART, QUART, nc.scalar.copy)
-            if s == 1 and c in stored:
-                c0, tiles, whole = stored[c]
-                rows_out = out[c0 * P : (c0 + tiles) * P, :].rearrange("(k p) j -> p k j", k=tiles)
-                nc.sync.dma_start(rows_out, whole[:])
+        def store(c0, tiles, whole, js):
+            rows_out = out[c0 * P : (c0 + tiles) * P, js].rearrange("(k p) j -> p k j", k=tiles)
+            nc.sync.dma_start(rows_out, whole[:, :, js])
+
+        groups = [(c, j0, HALF) for c in range(NT) for j0 in (0, HALF)][:-1]
+        groups = groups + [(NT - 1, HALF, QUART), (NT - 1, J - QUART, QUART)]
+        for n, (c, j0, width) in enumerate(groups):
+            acc = bank((n + 1) % Y_BANKS)[:, 0:width]
+            y_passes(acc, c, j0 // HALF, slice(j0 % HALF, j0 % HALF + width))
+            factor = ring.tile([P, width], F32, name="factor", bufs=4, align_bytes=64)
+            nc.scalar.activation(factor[:], acc, ACT.Identity, bias=bias1[:, c : c + 1])
+            nc.vector.tensor_tensor(result[c][:, j0 : j0 + width], listed(x0[c][:], j0, width), factor[:], MULT)
+            if j0 == HALF and 1 <= c <= 4:
+                quantise_up((c - 1) % 2, HALF + (c - 1) // 2 * QUART, QUART, False)
+            if j0 == HALF and c in stored:
+                store(*stored[c], slice(0, j0 + width))
+        store(*stored[NT - 1], slice(J - QUART, J))

@@ -310,6 +310,5 @@ def tile_list_xcross_relu_kernel(
             nc.vector.tensor_tensor(result[c][:, j0 : j0 + width], listed(x0[c][:], j0, width), factor[:], MULT)
             if j0 == HALF and 1 <= c <= 4:
                 quantise_up((c - 1) % 2, HALF + (c - 1) // 2 * QUART, QUART, False)
-            if j0 == HALF and c in stored:
-                store(*stored[c], slice(0, j0 + width))
-        store(*stored[NT - 1], slice(J - QUART, J))
+            if j0 + width == J and c in stored:
+                store(*stored[c], slice(0, J))

from contextlib import ExitStack

import concourse.mybir as mybir
from concourse.masks import make_identity

K, R, N, T, J = 1536, 1024, 1024, 2048, 1024
FLOPS = 2 * J * (K * R + K * N + R * N)

F32 = mybir.dt.float32
BF16 = mybir.dt.bfloat16
I32 = mybir.dt.int32
U32 = mybir.dt.uint32
U16 = mybir.dt.uint16
U8 = mybir.dt.uint8
FP8X4 = mybir.dt.float8_e4m3fn_x4
FP4X4 = mybir.dt.float4_e2m1fn_x4
ACT = mybir.ActivationFunctionType
MULT = mybir.AluOpType.mult
MAX = mybir.AluOpType.max

P = 128
KP = K // 512
RP = R // 512
NT = N // P
HALF = 512
QUART = 256
OWN_X0 = 5
LATE_WORDS = T + KP * N + RP * 4 * N + OWN_X0 * T
STORES = ((0, 5), (5, 2), (7, 1))
Y_BANKS = 4


def tile_list_xcross_relu_kernel(
    tc, tab_words, tab_scales, wb_words, wb_scales, dn_words, dn_scales, upw, x0T, b, offs, out
):
    nc = tc.nc
    with ExitStack() as ctx:
        keep = ctx.enter_context(tc.tile_pool(name="keep", bufs=1))
        ring = ctx.enter_context(tc.tile_pool(name="ring", bufs=2))
        psum = ctx.enter_context(tc.psum_pool(name="psum", bufs=1))

        def held(shape, dtype, name):
            return keep.tile(shape, dtype, name=name, align_bytes=64)

        def bank(n):
            return psum.tile([P, HALF], F32, name="bank%d" % n)

        offsets = keep.tile([P, J // 16], U16, name="offsets")
        v_moved = held([P, KP - 1, J // 4], I32, "v_moved")
        dn_plane = held([P, KP, R // 4], I32, "dn_plane")
        wb_plane = held([P, N // 4], I32, "wb_plane")
        b_rows = held([P, P], F32, "b_rows")
        ident = held([P, P], F32, "ident")
        dn_first = held([P, R // 2], I32, "dn_first")
        dn_rest = held([P, KP - 1, R // 2], I32, "dn_rest")
        dn_raw = [dn_first[:]] + [dn_rest[:, a - 1] for a in range(1, KP)]
        tab_win = [held([P, T], I32, "window%d" % a) for a in range(KP - 1)]
        with tc.tile_pool(name="head", bufs=1) as head_pool:
            space = head_pool.tile([P, LATE_WORDS], I32, name="space", align_bytes=64)
            tab_rows = space[:, 0 : T // 4]

            nc.gpsimd.memset(dn_plane[:], 0)
            nc.vector.memset(b_rows[:], 0.0)
            nc.vector.memset(wb_plane[:], 0)
            nc.vector.memset(v_moved[:], 0)
            dn_rows = dn_scales.rearrange("a (q r) n -> r q a n", r=4)
            make_identity(nc, ident[:])
            nc.gpsimd.dma_start(b_rows[0:NT, :], b.rearrange("(c p) -> c p", p=P))
            for q in range(4):
                nc.gpsimd.dma_start(
                    wb_plane[32 * q + 4 : 32 * q + 16, :], wb_scales[:, 4 * q : 4 * q + 4, :].bitcast(I32)
                )
            nc.sync.dma_start(offsets[:], offs)
            rows = tab_scales.rearrange("a q t -> (a q) t").bitcast(I32)
            for q in (0, 2, 1):
                nc.sync.dma_start(tab_rows[32 * q : 32 * q + 32, :], rows[4 * q : 4 * q + 32, :])
            nc.sync.dma_start(tab_rows[96:112, :], rows[12:28, :])
            nc.sync.dma_start(tab_rows[112:128, :], rows[32:48, :])

            def load_table(a):
                nc.sync.dma_start(tab_win[a][:], tab_words[a].rearrange("p t i -> p (t i)").bitcast(I32))

            load_table(0)
            nc.sync.dma_start(dn_first[:], dn_words[0].bitcast(I32))
            for r in range(4):
                nc.sync.dma_start(dn_plane[r:P:32], dn_rows[r].bitcast(I32))
            load_table(1)
            nc.sync.dma_start(dn_rest[:], dn_words[1:KP].rearrange("a p w -> p a w").bitcast(I32))

            def listed(window, j0, width):
                return window.indirect(offsets[:, j0 // 16 : (j0 + width) // 16])

            v_rows = held([P, J], U8, "v_rows")
            nc.vector.tensor_copy(v_rows[:], listed(tab_rows.bitcast(U8), 0, J))
        late = ctx.enter_context(tc.tile_pool(name="late", bufs=1))

        def late_tile(shape, dtype, name):
            return late.tile(shape, dtype, name=name, align_bytes=64)

        def move_rows(a):
            first_row = 16 if a == 1 else 112
            for r in range(4):
                nc.sync.dma_start(
                    v_moved[r:P:32, a - 1, :], v_rows[first_row + r : first_row + 16 : 4, :].bitcast(I32)
                )

        tab_win.append(late_tile([P, T], I32, "window2"))
        move_rows(1)
        load_table(2)
        move_rows(2)

        up_rows = upw.rearrange("(g p t) n -> g p (t n)", g=RP, t=4)
        up_raw = []
        for g in range(RP):
            raw = late_tile([P, 4 * N], F32, "up_raw%d" % g)
            nc.sync.dma_start(raw[:], up_rows[g])
            up_raw.append(raw[:].rearrange("p (t n) -> p t n", t=4))
        wb_rows = wb_words.rearrange("a p n i -> p a (n i)").bitcast(I32)
        wb = []
        x0 = []

        def load_wb(side):
            words = late_tile([P, KP, HALF], I32, "wb%d" % side)
            nc.sync.dma_start(words[:], wb_rows[:, :, side * HALF : (side + 1) * HALF])
            wb.append(words)

        def load_x0(c):
            if c < OWN_X0:
                win = late_tile([P, T], F32, "x0_%d" % c)
            elif c < NT - 1:
                win = held([P, T], F32, "window%d" % (c - OWN_X0))
            else:
                win = late_tile([P, T], F32, "window2")
            nc.sync.dma_start(win[:], x0T[c * P : (c + 1) * P, :])
            x0.append(win)

        for c in range(OWN_X0):
            if c % 4 == 0:
                load_wb(c // 4)
            load_x0(c)

        v_words = [[held([P, HALF], U32, "v_words0_%d" % a) for a in range(KP)], [None]]
        v_words[1].extend(held([P, HALF], U32, "v_words1_%d" % a) for a in range(1, KP))

        def gather(a, s, width=HALF):
            for j in range(0, HALF, width):
                nc.vector.tensor_copy(
                    v_words[s][a][:, j : j + width], listed(tab_win[a][:].bitcast(U32), s * HALF + j, width)
                )

        def v_plane(a, s):
            plane = v_rows[:] if a == 0 else v_moved[:, a - 1, :].bitcast(U8)
            return plane[:, s * HALF : (s + 1) * HALF]

        dn = [[held([P, HALF], U16, "dn%d_%d" % (a, g)) for g in range(RP)] for a in range(KP)]
        dn_scale = [[held([P, HALF], U8, "dn_scale%d_%d" % (a, g)) for g in range(RP)] for a in range(KP)]

        def deal_dn(a):
            for g in range(RP):
                nc.scalar.copy(
                    dn[a][g][:].rearrange("p (t b m) -> p b t m", t=4, m=8),
                    dn_raw[a].bitcast(U16)[:, g * HALF : (g + 1) * HALF].rearrange("p (b m t) -> p b t m", m=8, t=4),
                )
                nc.vector.tensor_copy(
                    dn_scale[a][g][:].rearrange("p (t b m) -> p b t m", t=4, m=16),
                    dn_plane[:, a, g * P : (g + 1) * P].bitcast(U8).rearrange("p (b m t) -> p b t m", m=16, t=4),
                )

        def dn_passes(acc, a, s, q, g, pair):
            js = slice(q * QUART, (q + 1) * QUART)
            for e in range(2):
                t = 2 * pair + e
                nc.tensor.matmul_mx(
                    acc[:, e * QUART : (e + 1) * QUART],
                    lhsT=dn[a][g][:, t * P : (t + 1) * P].bitcast(FP4X4),
                    lhsT_scale=dn_scale[a][g][:, t * P : (t + 1) * P],
                    rhs=v_words[s][a][:, js].bitcast(FP8X4),
                    rhs_scale=v_plane(a, s)[:, js],
                    start=(a == 0 and e == 0),
                    stop=(a == KP - 1 and e == 1),
                )

        h_words = [[None] * RP for s in range(2)]
        h_plane = [[held([P, HALF], U8, "h_plane%d_%d" % (s, g)) for g in range(RP)] for s in range(2)]
        up_codes = {}

        def quantise(words, plane, grouped):
            nc.vector.quantize_mx(out=words.bitcast(FP8X4), scales=plane, in_=grouped)

        def quantise_up(g, n0, width, on_vector):
            if on_vector:
                grouped = held([P, width, 4], BF16, "stage")
            else:
                grouped = ring.tile([P, width, 4], BF16, name="factor", bufs=4, align_bytes=64)
            copy = nc.vector.tensor_copy if on_vector else nc.scalar.copy
            copy(
                grouped[:].rearrange("p (c i) t -> p c t i", i=4),
                up_raw[g][:, :, n0 : n0 + width].rearrange("p t (c i) -> p c t i", i=4),
            )
            words = held([P, width], U32, "up_words%d_%d" % (g, n0))
            plane = held([P, width], U8, "up_plane%d_%d" % (g, n0))
            quantise(words[:], plane[:], grouped[:].rearrange("p c t -> p (c t)"))
            for at in range(0, width, P):
                up_codes[g, (n0 + at) // P] = (words[:, at : at + P], plane[:, at : at + P])

        def relu(grouped, acc, q, pair):
            dst = grouped[:, q * QUART : (q + 1) * QUART, 2 * pair : 2 * pair + 2]
            nc.scalar.activation(dst, acc[:].rearrange("p (e j) -> p j e", e=2), ACT.Relu)

        def h_tile(s, g):
            return held([P, HALF, 4], BF16, "h%d_%d" % (s, g))

        def quantise_h(s, g, grouped):
            name = "stage" if (s, g) == (1, 1) else "h_words%d_%d" % (s, g)
            h_words[s][g] = held([P, HALF], U32, name)
            quantise(h_words[s][g][:], h_plane[s][g][:], grouped[:].rearrange("p j t -> p (j t)"))

        slots = [(g, u) for half in range(2) for g in range(RP) for u in (2 * half, 2 * half + 1)]
        first = {slot: bank(n) for n, slot in enumerate(slots)}
        for a in range(KP):
            deal_dn(a)
            gather(a, 0, HALF if a == 1 else QUART)
            for g, u in slots:
                js = slice(u * P, (u + 1) * P)
                for t in range(4):
                    nc.tensor.matmul_mx(
                        first[g, u][:, t * P : (t + 1) * P],
                        lhsT=dn[a][g][:, t * P : (t + 1) * P].bitcast(FP4X4),
                        lhsT_scale=dn_scale[a][g][:, t * P : (t + 1) * P],
                        rhs=v_words[0][a][:, js].bitcast(FP8X4),
                        rhs_scale=v_plane(a, 0)[:, js],
                        start=(a == 0 and t == 0),
                        stop=(a == KP - 1 and t == 3),
                    )
        v_words[1][0] = held([P, HALF], U32, "dn_plane")
        for a in range(KP):
            gather(a, 1)
        for c in range(OWN_X0, NT):
            load_x0(c)
        grouped = [h_tile(0, g) for g in range(RP)]
        for g, u in slots:
            dst = grouped[g][:, u * P : (u + 1) * P, :]
            src = first[g, u][:].rearrange("p (t j) -> p j t", t=4)
            if g == 1:
                nc.vector.tensor_scalar(dst, src, 0.0, None, MAX)
            else:
                nc.scalar.activation(dst, src, ACT.Relu)
        for g in range(RP):
            quantise_h(0, g, grouped[g])
        quantise_up(0, 0, HALF, True)
        quantise_up(1, 0, QUART, True)
        quantise_up(1, QUART, QUART, True)
        pairs = [h_tile(1, g) for g in range(RP)]

        def second_half(g, n):
            q, pair = divmod(n, 2)
            acc = bank(4 * g + n)
            for a in range(KP):
                dn_passes(acc, a, 1, q, g, pair)
            relu(pairs[g], acc, q, pair)
            if n == 3:
                quantise_h(1, g, pairs[g])

        for n in range(4):
            second_half(0, n)
        b_t = bank(0)
        nc.tensor.transpose(b_t[:, 0:P], b_rows[:], ident[:])
        bias1 = held([P, NT], F32, "bias1")
        nc.scalar.activation(bias1[:], b_t[:, 0:NT], ACT.Identity, bias=1.0)
        for n in range(4):
            second_half(1, n)

        result = []
        stored = {}
        for c0, tiles in STORES:
            whole = held([P, tiles, J], F32, "result%d" % c0)
            result.extend(whole[:, k] for k in range(tiles))
            stored[c0 + tiles - 1] = (c0, tiles, whole)

        def y_passes(acc, c, s, js):
            cols = slice(c * P, (c + 1) * P)
            for k in range(KP + RP):
                if k < KP:
                    operands = (wb[c // 4][:, k, c % 4 * P : (c % 4 + 1) * P], wb_plane[4 * k + 4 : P, :].bitcast(U8)[:, cols])
                    operands = operands + (v_words[s][k][:, js], v_plane(k, s)[:, js])
                else:
                    g = k - KP
                    operands = up_codes[g, c] + (h_words[s][g][:, js], h_plane[s][g][:, js])
                nc.tensor.matmul_mx(
                    acc,
                    lhsT=operands[0].bitcast(FP8X4),
                    lhsT_scale=operands[1],
                    rhs=operands[2].bitcast(FP8X4),
                    rhs_scale=operands[3],
                    start=(k == 0),
                    stop=(k == KP + RP - 1),
                )

        def store(c0, tiles, whole, js):
            rows_out = out[c0 * P : (c0 + tiles) * P, js].rearrange("(k p) j -> p k j", k=tiles)
            nc.sync.dma_start(rows_out, whole[:, :, js])

        groups = [(c, j0, HALF) for c in range(NT) for j0 in (0, HALF)][:-1]
        groups = groups + [(NT - 1, HALF, QUART), (NT - 1, J - QUART, QUART)]
        for n, (c, j0, width) in enumerate(groups):
            acc = bank((n + 1) % Y_BANKS)[:, 0:width]
            y_passes(acc, c, j0 // HALF, slice(j0 % HALF, j0 % HALF + width))
            factor = ring.tile([P, width], F32, name="factor", bufs=4, align_bytes=64)
            nc.scalar.activation(factor[:], acc, ACT.Identity, bias=bias1[:, c : c + 1])
            nc.vector.tensor_tensor(result[c][:, j0 : j0 + width], listed(x0[c][:], j0, width), factor[:], MULT)
            if j0 == HALF and 1 <= c <= 4:
                quantise_up((c - 1) % 2, HALF + (c - 1) // 2 * QUART, QUART, False)
            if j0 + width == J and c in stored:
                store(*stored[c], slice(0, J))
